import numpy as np, ml_dtypes
CORES = [48,51,52,55]
N = 4
import mx_ref
BF = ml_dtypes.bfloat16
def pick(q, e):
    c = np.concatenate([q[0].reshape(128, -1, 4), np.zeros((128, 1, 4), np.uint8)], axis=1); s = np.concatenate([q[1], np.ones((16, 1), np.uint8)], axis=1)
    return (np.ascontiguousarray(c[:, e].reshape(128, -1)), np.ascontiguousarray(s[:, e]))
def join(*qs):
    return (np.concatenate([q[0] for q in qs], axis=1), np.concatenate([q[1] for q in qs], axis=1))
def put(q, e, v):
    c, s = q[0].reshape(128, -1, 4).copy(), q[1].copy(); c[:, e] = v[0].reshape(128, -1, 4); s[:, e] = v[1]
    return (c.reshape(128, -1), s)
def pk(c, s):
    return (np.ascontiguousarray(c), mx_ref.live(s))
def emit(q):
    return q[0], q[1]
def decode(q):
    o = []
    for b in range(4):
        e = np.zeros((128, 128, 4), np.float32); e[np.arange(128), np.arange(128), b] = 1
        o.append(mx_ref.matmul(mx_ref.quantize(e.reshape(128, 512).astype(BF)), q))
    return np.stack(o, axis=2).reshape(128, -1)
def f(rng, *shape):
    return mx_ref.flush((rng.standard_normal(shape, dtype=np.float32) * np.exp2(rng.integers(-2, 3, shape[:-1] + (1,)))).astype(BF))
def wide(rng, *shape, cols=0):
    v = rng.standard_normal(shape, dtype=np.float32) * np.exp2(rng.integers(-12, 13, shape)).astype(np.float32)
    if cols: v *= np.repeat(np.exp2(rng.integers(-cols, cols + 1, shape[:-2] + (1, shape[-1] // 4))) * (rng.random(shape[:-2] + (1, shape[-1] // 4)) > 0.0625), 4, axis=-1).astype(np.float32)
    return mx_ref.flush(v.astype(BF))
T, CAPP = 192, 48
def quads(q, e):
    c = np.concatenate([q[0].reshape(128, -1, 4), np.zeros((128, 1, 4), np.uint8)], axis=1); s = np.concatenate([q[1], np.ones((16, 1), np.uint8)], axis=1)
    return (np.concatenate([c[32 * h:32 * h + 32][:, e[h]] for h in range(4)]).reshape(128, -1), np.concatenate([s[4 * h:4 * h + 4][:, e[h]] for h in range(4)]))
def level(b, z):
    n, e = z[1].shape[1], []
    for h in range(4):
        only = np.where(np.arange(4)[:, None] == h, np.arange(n)[None, :], -1)
        e.append(np.argmax(mx_ref.matmul(b, quads(z, only)) + np.float32(0), axis=0))
    e = np.stack(e)
    return e, quads(b, e)
def big(v):
    v = v.astype(np.float32)
    v[np.abs(v) < np.float32(2.0 ** -16)] = 0
    return v.astype(BF)
def coarse(v):
    v = v.copy()
    v[:, N:] = 0
    return np.stack([v.reshape(128, 512)] * N)
def planted(rng, cell, low=False):
    at = rng.permutation(N)[np.arange(128) // (128 // N)]
    c = (1 + rng.random((128, 128, 4))) * (at[:, None] == np.arange(128)[None, :])[:, :, None]
    on = at[None, :, None] == cell[:, None, :]
    v = np.where(on[:, :, :, None], 8 + 8 * rng.random((N, 128, T, 4)), 2 * rng.random((N, 128, T, 4)) - 1)
    if low:
        u = 1 + rng.random((N, 128, T // 2, 4))
        v[:, :, 1::2] = np.where(on[:, :, 1::2, None], -0.5 * u, -8 * u)
        c = c * 2.0 ** 20
    v = v * np.exp2(rng.integers(-3, 4, (N, 1, T, 1)))
    return {"x": big(v.reshape(N, 128, 4 * T)), "co": coarse(big(c))}
def setup_inputs(rng):
    return {"x": big(f(rng, N, 128, 4 * T)), "co": coarse(big(f(rng, 128, 512)).reshape(128, 128, 4)), "b1": big(f(rng, N, 128, 512)), "b2": big(f(rng, N, 128, 512)), "w": f(rng, N, 128, 512)}
def setup_inputs_spread(rng):
    d = setup_inputs(rng)
    d["x"], d["b1"] = big(wide(rng, N, 128, 4 * T, cols=6)), big(wide(rng, N, 128, 512))
    return d
def setup_inputs_ties(rng):
    d = setup_inputs(rng)
    for k in ("b1", "b2"):
        b = d[k].reshape(N, 128, 128, 4).copy()
        for r in range(N):
            for h in range(4): b[r, 32 * h:32 * h + 32] = b[r, 32 * h:32 * h + 32][:, rng.permutation(128) % 32]
        d[k] = b.reshape(N, 128, 512)
    c = d["co"][0].reshape(128, 128, 4).copy()
    c[:, :N] = c[:, rng.permutation(N) % (N // 2)]
    d["co"] = coarse(c)
    return d
def setup_inputs_crowd(rng):
    g, cell = int(rng.integers(0, N)), []
    for s in range(N):
        o = rng.permutation(np.delete(np.arange(N), g))
        if o[0] == s: o = o[::-1]
        m = int(rng.integers(1, 17))
        cell.append(rng.permutation(np.concatenate([np.full(CAPP + m, g), np.full(CAPP, o[0]), o[1:][rng.integers(0, N - 2, T - 2 * CAPP - m)]])))
    return {**setup_inputs(rng), **planted(rng, np.stack(cell))}
def setup_inputs_few(rng):
    g, a, b = [int(i) for i in rng.permutation(N)[:3]]
    cell = np.delete(np.arange(N), g)[rng.integers(0, N - 1, (N, T))]
    cell[a], cell[b] = a, a
    return {**setup_inputs(rng), **planted(rng, cell, low=True)}
def setup_inputs_zero(rng):
    d, h = setup_inputs(rng), [int(i) for i in rng.permutation(4)]
    neg, pat, gap = [slice(32 * i, 32 * i + 32) for i in h[:3]]
    p = (1 + rng.random((32, 1, 4))) * np.exp2(rng.integers(-2, 3, (32, 1, 1)))
    v, b, c = d["x"].astype(np.float32).reshape(N, 128, T, 4), d["b1"].astype(np.float32).reshape(N, 128, 128, 4), d["co"][0].reshape(128, 128, 4).copy()
    u = d["b2"].astype(np.float32)
    c[neg], c[pat] = 0, 0
    c[:, int(rng.integers(0, N))] = 0
    v[:, neg], b[:, neg], u[:, neg] = -np.abs(v[:, neg]), np.abs(b[:, neg]), np.abs(u[:, neg])
    v[:, pat] = p
    for r in range(N):
        e, k = rng.permutation(T), rng.integers(0, 4, 128)
        v[r, gap][:, e[T // 8:T // 2]] = 0
        v[r][:, e[:T // 8]] = 0
        k[int(rng.integers(0, 128))] = 0
        b[r, pat] = p * np.exp2(-k.astype(np.float64))[:, None]
        if r % 2 == 0: b[r, neg, int(rng.integers(0, 128))] = 0
    k = np.float32(2.0 ** 20)
    d["x"], d["b1"], d["b2"], d["co"] = big(v.reshape(N, 128, 4 * T) * k), big(b.reshape(N, 128, 512) * k), big(u * k), coarse(c)
    return d
def check_inputs(d):
    b = []
    for k in ("x", "co", "b1", "b2", "w"):
        v = np.abs(d[k].astype(np.float32))
        if not (np.isfinite(v).all() and ((v == 0) | (v >= 2.0 ** -30) & (v <= 2.0 ** 30)).all()): b.append("a value of " + k)
    c = d["co"].astype(np.float32)
    if (c[:, :, 4 * N:] != 0).any(): b.append("co has numbers behind its first N columns")
    if (c != c[:1]).any(): b.append("co isn't the same on all ranks")
    return b
def reference(x, co, b1, b2, w):
    oc, osc = np.zeros((N, 128, 8 * T), np.uint8), np.zeros((N, 16, 2 * T), np.uint8)
    wn, y = np.full((N, 8, T), -1, np.float32), np.zeros((N, 128, T), np.float32)
    q = [mx_ref.quantize(x[s]) for s in range(N)]
    taken = np.full((N, N, CAPP), -1)
    for s in range(N):
        cell = np.argmax(mx_ref.matmul(mx_ref.quantize(co[s]), q[s])[:N] + np.float32(0), axis=0)
        for d in range(N):
            t = np.flatnonzero(cell == d)[:CAPP]
            taken[s, d, :len(t)] = t
    home = [pick(q[s], np.full(2 * T, -1)) for s in range(N)]
    for d in range(N):
        z = join(*[pick(q[s], taken[s, d]) for s in range(N)])
        n1, v1 = level(mx_ref.quantize(b1[d]), z)
        r = mx_ref.quantize((decode(z) - decode(v1)).astype(BF))
        n2, v2 = level(mx_ref.quantize(b2[d]), r)
        for s in range(N):
            k = np.flatnonzero(taken[s, d] >= 0)
            t, i = taken[s, d][k], s * CAPP + k
            wn[s, :4, t], wn[s, 4:, t] = n1[:, i].T, n2[:, i].T
            home[s] = put(put(home[s], t, pick(v1, i)), T + t, pick(v2, i))
    for s in range(N):
        oc[s], osc[s] = emit(home[s])
        m = mx_ref.matmul(mx_ref.quantize(w[s]), home[s])
        y[s] = m[:, :T] + m[:, T:]
    return {"oc": oc, "osc": osc, "wn": wn, "y": y}

@@ -1,0 +1,472 @@
+from concourse.bass import DstId, RemoteDMATransfer
+from concourse.mybir import dt, AluOpType, AxisListType, ActivationFunctionType
+
+A = AluOpType
+F = ActivationFunctionType
+NR = 4
+LOW = -1e29
+RND = 1.5 * 2.0 ** 27
+
+
+def _codes(n):
+    return ("sbuf", [128, n], "float8_e4m3fn_x4")
+
+
+def _plane(n):
+    return ("sbuf", [128, n], "uint8")
+
+
+def _sb(n, d):
+    return ("sbuf", [128, n], d)
+
+
+SCRATCH = {}
+for _n, _w in (("xq", 192), ("cq", 134), ("wq", 128), ("p1q", 128), ("b1q", 512), ("b2q", 512), ("trq", 256), ("wlq", 128), ("epq", 512),
+               ("otq", 134), ("abq", 140), ("xaq", 136), ("xcq", 132), ("xpq", 140), ("zsq", 144), ("zq", 192), ("vbq", 192), ("lvq", 208),
+               ("v2q", 144), ("lwq", 208), ("raq", 128), ("rcq", 128), ("o1q", 192), ("o2q", 192)):
+    SCRATCH[_n] = _codes(_w)
+    SCRATCH[_n + "s"] = _plane(_w)
+for _n, _w in (("xb", 768), ("cb", 536), ("wb", 512), ("pb1", 512), ("pb2", 512), ("bm1", 2048), ("bm2", 2048), ("trb", 516), ("wlb", 512),
+               ("epb", 516), ("ot", 536), ("ab", 560), ("xa", 544), ("xc", 528), ("xp", 560), ("rt", 768), ("zz", 536), ("on1", 128),
+               ("t1", 128), ("im", 128), ("jk1", 1024), ("jk2", 1024), ("nbf", 16), ("ln", 128), ("tr", 128)):
+    SCRATCH[_n] = _sb(_w, "bfloat16")
+for _n, _w in (("rst", 10), ("rma", 10), ("ua", 11), ("rr", 10), ("hc", 2), ("nl", 2), ("tk", 4), ("tkn", 2), ("ib", 12), ("abx", 12),
+               ("vl", 1), ("mk", 4), ("hcol", 1), ("df", 1), ("e0", 1), ("e4", 1), ("off", 2), ("rm1", 1024), ("rm2", 1024), ("nf", 80),
+               ("tf", 2), ("q1", 2), ("wt", 208), ("wno", 192), ("ysb", 192), ("db", 512), ("dq", 384), ("g2", 192), ("g3", 192)):
+    SCRATCH[_n] = _sb(_w, "float32")
+for _n, _w in (("pi", 1), ("pa", 1), ("pb", 1), ("gi", 1), ("ui", 1), ("ti", 1), ("hi", 1), ("vi", 2), ("ai", 2), ("bi", 2)):
+    SCRATCH[_n] = _sb(_w, "int32")
+for _n, _w in (("zl", 12), ("zl2", 4), ("pl", 12), ("l1", 12), ("l2", 12), ("l2b", 4), ("ofo", 2), ("ofa", 8)):
+    SCRATCH[_n] = _sb(_w, "uint16")
+for _n in ("psa", "psb", "psc", "psd", "pd0", "pd1", "pd2", "pd3"):
+    SCRATCH[_n] = ("psum", [128, 512], "float32")
+SEMAPHORES = ["qv", "qs", "qt", "qg", "dx", "dco", "dp1", "dp2", "db2", "dep", "dw", "dz", "dv", "do", "st", "zin", "vin", "win", "nin", "oin",
+              "left"]
+
+
+def _mask(topo, src, peers):
+    out, far, near = {}, 0, 0
+    for c in peers:
+        e = topo.engines(src, c)
+        if topo.die(src) != topo.die(c):
+            out[c] = e[far * 8:far * 8 + 8:2]
+            far += 1
+        else:
+            out[c] = e[1 + near * 8:9 + near * 8:2]
+            near += 1
+    return out
+
+
+def rank_program(g, core, T, topo):
+    rank = T.rank_of(core)
+    if rank is None:
+        return
+    S = T.sem
+    eng = {"v": g.vector, "s": g.scalar, "t": g.tensor, "g": g, "y": g.sync}
+    qsem = {"v": "qv", "s": "qs", "t": "qt", "g": "qg"}
+    cnt = {"v": 0, "s": 0, "t": 0, "g": 0}
+    seen = {q: {} for q in eng}
+
+    def need(q, *deps):
+        for sem, val in deps:
+            if seen[q].get(sem, 0) < val:
+                eng[q].wait_ge(S[sem], val)
+                seen[q][sem] = val
+
+    def done(q, ins):
+        ins.then_inc(S[qsem[q]], 1)
+        cnt[q] += 1
+        return (qsem[q], cnt[q])
+
+    V, SC, TE = g.vector, g.scalar, g.tensor
+    stores = [0]
+
+    def dma(q, out, in_, sem):
+        eng[q].dma_start(out, in_).then_inc(S[sem], 16)
+        if sem == "st":
+            stores[0] += 1
+
+    def ts(out, in0, s1, s2, op0, op1, *deps):
+        need("v", *deps)
+        if op1 is None:
+            return done("v", V.tensor_scalar(out, in0, s1, s2, op0))
+        return done("v", V.tensor_scalar(out, in0, s1, s2, op0, op1))
+
+    def tt(out, a, b, op, *deps):
+        need("v", *deps)
+        return done("v", V.tensor_tensor(out, a, b, op))
+
+    def fill(ap, c, *deps):
+        need("v", *deps)
+        return done("v", V.memset(ap, c))
+
+    def copy(out, in_, *deps):
+        need("v", *deps)
+        return done("v", V.tensor_copy(out, in_))
+
+    def quant(q, s, in_, *deps):
+        need("v", *deps)
+        return done("v", V.quantize_mx(q, s, in_))
+
+    def act(out, in_, func, *deps):
+        need("s", *deps)
+        return done("s", SC.activation(out, in_, func))
+
+    def mm(out, name, c0, c1, mov, m0, m1, start, stop, *deps):
+        need("t", *deps)
+        return done("t", TE.matmul_mx(out, T[name][:, c0:c1], T[name + "s"][:, c0:c1], T[mov][:, m0:m1], T[mov + "s"][:, m0:m1], start, stop))
+
+    def pick_codes(dst, d0, d1, win, w1, lst, *deps):
+        need("v", *deps)
+        return done("v", V.tensor_copy(T[dst][:, d0:d1].bitcast(dt.uint32), T[win][:, 0:w1].bitcast(dt.uint32).indirect(lst)))
+
+    def pick_scales(dst, d0, d1, win, w1, lst, *deps):
+        return act(T[dst + "s"][:, d0:d1], T[win + "s"][:, 0:w1].indirect(lst), F.Copy, *deps)
+
+    def pick(*a):
+        return pick_codes(*a), pick_scales(*a)
+
+    peers = [T.cores[(rank + 1 + a) % NR] for a in range(3)]
+    emask = _mask(topo, core, peers)
+    landing = sum(len(_mask(topo, c, [T.cores[(T.rank_of(c) + 1 + a) % NR] for a in range(3)])[core]) for c in peers)
+    left = [0]
+
+    def fan(srcs, dsts, sem, *deps):
+        need("g", *deps)
+        tr = []
+        for a, c in enumerate(peers):
+            rid, pid, _ = topo.addr(c)
+            tr.append(RemoteDMATransfer(dst_ids=[DstId(rid=rid, pnc=pid)], dma_engine_mask=sum(1 << e for e in emask[c]),
+                                        remote_sem=S[sem], srcs=[srcs[a]], dsts=[dsts[a]]))
+            left[0] += len(emask[c])
+        g.remote_dma_fused(tr, local_sem=S["left"])
+
+    def fan_codes(src, dst, sem, *c):
+        fan([T[src][:, 48 * a:48 * a + 48].bitcast(dt.uint8) for a in range(3)],
+            [T[dst][:, 48 * (2 - a):48 * (2 - a) + 48].bitcast(dt.uint8) for a in range(3)], sem, *c)
+
+    def fan_scales(src, dst, sem, *c):
+        fan([T[src + "s"][:, 48 * a:48 * a + 48] for a in range(3)], [T[dst + "s"][:, 48 * (2 - a):48 * (2 - a) + 48] for a in range(3)], sem, *c)
+
+    dma("y", T.xb[:], T.x[:], "dx")
+    dma("s", T.cb[:, 24:40], T.co[:, 0:4 * NR], "dco")
+    dma("y", T.pb1[:], T.b1[:], "dp1")
+
+    c_pi = done("g", g.iota(T.pi[:], [[0, 1]], 0, 1))
+    c_on = fill(T.on1[:], 1.0)
+    c_zz = fill(T.zz[:], 0.0)
+    need("y", c_zz)
+    dma("y", T.epb[:], T.zz[:, 0:516], "dep")
+    dma("y", T.pb2[:], T.b2[:], "dp2")
+    need("s", c_zz)
+    c_tr = done("s", SC.activation(T.trb[:], T.zz[:, 0:516], F.Identity, bias=1.0))
+    c_ot = act(T.ot[:], T.zz[:], F.Copy)
+    need("g", c_on)
+    c_t1 = done("g", g.affine_select(T.t1[:], T.on1[:], [[1, 128]], A.is_gt, 0.0, 0, -1))
+    c_cb = done("g", g.iota(T.cb[:, 40:536], [[0, 496]], 0, 0, allow_small_or_imprecise_dtypes=True))
+    ts(T.gi[:], T.pi[:], 4, None, A.arith_shift_right, None, c_pi)
+    c = ts(T.ui[:], T.pi[:], 2, 3, A.arith_shift_right, A.bitwise_and)
+    ts(T.ti[:], T.pi[:], 3 if rank < 2 else 0, None, A.bitwise_and, None)
+    c_hi = ts(T.hi[:], T.pi[:], 5, None, A.arith_shift_right, None)
+    c = tt(T.df[:], T.gi[:], T.ui[:], A.subtract, c)
+    c_cb0 = fill(T.cb[:, 0:24], 0.0)
+    for h in range(4):
+        c_mk = ts(T.mk[:, h:h + 1], T.hi[:], float(h), None, A.is_equal, None, c_hi)
+    if rank % 2 == 0:
+        ts(T.e0[:], T.df[:], 0.0, None, A.is_equal, None, c)
+    c = ts(T.e4[:], T.df[:], 4.0, None, A.is_equal, None, c)
+    c_tr = fill(T.trb[:, 2:516:4], 0.0, c_tr)
+    for k, (e, v) in enumerate((((T.e0, -8.0), (T.e4, -8.0)), ((T.e4, -4.0),))[rank % 2]):
+        c = ts(T.off[:, k:k + 1], T.ti[:], v, e[:], A.add, A.mult, c)
+    wide = 2 - rank % 2
+    c_rs = fill(T.rst[:], 0.0)
+    c_of = ts(T.ofo[:, 0:wide], T.off[:, 0:wide], 8.0, None, A.add, None, c)
+    c_rs = fill(T.rst[:, 4:7], LOW, c_rs)
+    need("g", c_t1, c_tr)
+    c_tri = done("g", g.affine_select(T.trb[:, 1:513:4], T.t1[:], [[1, 128]], A.not_equal, 1024.0, 0, -1))
+    need("g", c_ot)
+    c_oi = done("g", g.iota(T.ot[:, 27:75:4], [[0, 2], [2, 6]], 0, 0, allow_small_or_imprecise_dtypes=True))
+    own = slice(2 * rank, 2 * rank + wide)
+    fan([T.ofo[:, 0:wide]] * 3, [T.ofa[:, own]] * 3, "oin", c_of)
+    need("y", c_of)
+    dma("y", T.ofa[:, own], T.ofo[:, 0:wide], "do")
+    if rank < NR - 1:
+        done("g", g.iota(T.ib[:, 0:9 - 3 * rank], [[256, 3 - rank], [16, 3]], 1280 + 256 * rank, 0, allow_small_or_imprecise_dtypes=True))
+    c_ib = done("g", g.iota(T.ib[:, 9 - 3 * rank:12], [[256, rank + 1], [16, 3]], 1024, 0, allow_small_or_imprecise_dtypes=True))
+    c_im = done("g", g.iota(T.im[:], [[0, 8], [1, 16]], 0, 0, allow_small_or_imprecise_dtypes=True))
+    need("g", ("dep", 16))
+    c_ep = done("g", g.affine_select(T.epb[:, 4:516:4], T.on1[:], [[1, 128]], A.is_equal, 0.0, 0, -1))
+    c_w0 = act(T.wlb[:], T.zz[:, 0:512], F.Copy)
+    c_xp = act(T.xp[:, 96:560], T.zz[:, 0:464], F.Copy)
+
+    def masked(bm, pb, h):
+        return done("s", SC.activation(bm[:, 512 * h:512 * h + 512], pb[:], F.Copy, scale=T.mk[:, h:h + 1]))
+    need("s", c_mk, ("dp1", 16))
+    for h in range(3):
+        masked(T.bm1, T.pb1, h)
+
+    c_q = quant(T.cq[:], T.cqs[:], T.cb[:], ("dco", 16), c_cb, c_cb0)
+    c_x = quant(T.xq[:], T.xqs[:], T.xb[:], ("dx", 16))
+    need("y", c_q)
+    for b in ("lvq", "lwq"):
+        dma("y", T[b][:, 192:208].bitcast(dt.uint8), T.cq[:, 64:80].bitcast(dt.uint8), "dz")
+        dma("y", T[b + "s"][:, 192:208], T.cqs[:, 64:80], "dz")
+    mm(T.psa[:, 0:128], "xq", 0, 128, "cq", 6, 134, True, False, c_x)
+    m = mm(T.psa[:, 0:128], "xq", 64, 192, "cq", 0, 128, False, True)
+    c_ua = fill(T.ua[:], 0.0)
+    c_vl = ts(T.vl[:], T.pi[:], 64.0, None, A.is_ge, None)
+    c_o1 = fill(T.ot[:, 1:64:4], -7.5 / 128, c_ot)
+    for k in range(2):
+        quant(T.trq[:, 128 * k:128 * k + 128], T.trqs[:, 128 * k:128 * k + 128], T.trb[:, 1 + 2 * k:513 + 2 * k], c_tri)
+
+    def scan(out, d0, d1, *deps):
+        need("v", *deps)
+        return done("v", V.tensor_tensor_scan(out, d0, d1, LOW, A.add, A.max))
+    s = scan(T.rma[:], T.rst[:], T.psa[:, 0:10], m, c_rs)
+    ts(T.pa[:], T.pi[:], 112, None, A.bitwise_and, None)
+    u = ts(T.ua[:, 1:5], T.rma[:, 0:4], T.rma[:, 3:4], None, A.is_equal, None, s, c_ua)
+    u = ts(T.ua[:, 7:11], T.rma[:, 6:10], T.rma[:, 9:10], T.vl[:], A.is_equal, A.mult, c_vl)
+    c_pb = ts(T.pb[:], T.pi[:], 15, None, A.bitwise_and, None)
+    o = tt(T.ot[:, 24:64:4], T.ua[:, 1:11], T.ua[:, 0:10], A.subtract, u, c_o1)
+    c_o = quant(T.otq[:], T.otqs[:], T.ot[:], o, c_oi)
+    mm(T.psc[:, 0:128], "trq", 0, 128, "otq", 6, 134, True, False, c_o)
+    m = mm(T.psc[:, 0:128], "trq", 128, 256, "otq", 0, 128, False, True)
+    ts(T.tk[:, 2:3], T.pa[:], 64.0, T.vl[:], A.add, A.mult, c_pb)
+    c = ts(T.tk[:, 3:4], T.pb[:], T.vl[:], None, A.mult, None)
+    copy(T.tk[:, 0:1], T.pa[:])
+    c_tk = copy(T.tk[:, 1:2], T.pb[:])
+    c_tn = ts(T.tkn[:], T.tk[:, 2:4], -0.0625, None, A.mult, None, c)
+    c_ln = fill(T.ln[:], 0.0)
+    r = scan(T.rr[:], T.rst[:], T.psc[:, 0:10], m)
+    c_hc = ts(T.hc[:], T.rr[:, 3:10:6], RND, RND, A.add, A.subtract, r)
+    need("s", c_hc, c_ib, c_tn)
+    c = done("s", SC.activation(T.abx[:], T.ib[:], F.Abs, bias=T.hc[:, 1:2], scale=-1.0))
+    need("s", c)
+    for t in (2, 3):
+        c_b = done("s", SC.activation(T.ab[:, 512 + t:560:4], T.abx[:], F.Relu, bias=T.tk[:, t:t + 1], scale=T.tkn[:, t - 2:t - 1]))
+    c_m1 = masked(T.bm1, T.pb1, 3)
+    c_nl = tt(T.nl[:], T.hc[:], T.rr[:, 3:10:6], A.subtract, c_hc)
+    for t in range(2):
+        ts(T.ab[:, 512 + t:560:4], T.ib[:], T.hc[:, 0:1], T.tk[:, t:t + 1], A.is_equal, A.mult, c_tk, c_ib)
+    for t in range(4):
+        c_a = ts(T.ab[:, t:512:4], T.im[:], T.nl[:, t // 2:t // 2 + 1], 7.5, A.subtract, A.is_equal, c_nl, c_im) if False else \
+            ts(T.ab[:, t:512:4], T.im[:], T.nl[:, t // 2:t // 2 + 1], 7.5, A.add, A.is_equal, c_nl, c_im)
+    c_a = quant(T.abq[:], T.abqs[:], T.ab[:], c_a, c_b)
+    m0 = mm(T.psa[:, 0:128], "abq", 0, 128, "abq", 12, 140, True, True, c_a)
+
+    def e_tile(b):
+        return quant(T.epq[:, 128 * b:128 * b + 128], T.epqs[:, 128 * b:128 * b + 128], T.epb[:, 4 - b:516 - b], c_ep)
+    c_e = [e_tile(0), e_tile(1)]
+    c_l = copy(T.zl[:, 0:9], T.psa[:, 116:125], m0)
+    zv, zs = pick("zsq", 0, 144, "xq", 192, T.zl[:, 0:9], c_l)
+    fan_codes("zsq", "zq", "zin", zv, c_ln)
+    fan_scales("zsq", "zq", "zin", zs)
+    c_l = copy(T.zl2[:, 0:3], T.psa[:, 125:128])
+    c_p1 = quant(T.p1q[:], T.p1qs[:], T.pb1[:], ("dp1", 16))
+    zo = pick("zq", 144, 192, "xq", 192, T.zl2[:, 0:3], c_l)
+
+    c_xc = done("g", g.iota(T.xc[:, 32:528], [[0, 496]], 0, 0, allow_small_or_imprecise_dtypes=True))
+    for h in range(2):
+        c_g = done("g", g.iota(T.bm2[:, 512 * h:512 * h + 512], [[0, 512]], 0, 0, allow_small_or_imprecise_dtypes=True))
+    need("y", c_g)
+    for h in range(2):
+        dma("y", T.bm2[32 * h:32 * h + 32, 512 * h:512 * h + 512], T.b2[32 * h:32 * h + 32, :], "db2")
+    dma("y", T.wb[:], T.w[:], "dw")
+    c_db = []
+
+    def table(b):
+        m = mm(T["pd%d" % b][:, 0:128], "epq", 128 * b, 128 * b + 128, "p1q", 0, 128, True, True, c_e[b], c_p1)
+        need("s", m)
+        c_db.append(done("s", SC.activation(T.db[:, 128 * b:128 * b + 128], T["pd%d" % b][:, 0:128], F.Copy, scale=-1.0)))
+    table(0)
+    table(1)
+    c_xa = act(T.xa[:, 64:544], T.zz[:, 0:480], F.Copy)
+    c_e.append(e_tile(2))
+    c_e.append(e_tile(3))
+    table(2)
+    table(3)
+    c_b1 = quant(T.b1q[:], T.b1qs[:], T.bm1[:], c_m1)
+    need("s", ("dp2", 16))
+    for h in (2, 3):
+        c_m2 = masked(T.bm2, T.pb2, h)
+    c_f = fill(T.nf[:], 0.0)
+    for t in range(4):
+        c_w = ts(T.wlb[:, 129 * t:128 * t + 128:4], T.im[:, 0:32], T.tk[:, 1:2], None, A.is_equal, None, c_w0)
+    c = ts(T.vi[:], T.rr[:, 3:10:6], -1016.5 + 256 * (3 - rank), None, A.add, None)
+    c_w = quant(T.wlq[:], T.wlqs[:], T.wlb[:], c_w)
+    ts(T.ai[:], T.vi[:], 8, 3, A.arith_shift_right, A.bitwise_and, c)
+    c_bi = ts(T.bi[:], T.vi[:], 255, None, A.bitwise_and, None)
+    c_hcol = ts(T.hcol[:], T.hi[:], 128.0, None, A.mult, None)
+
+    where = ((("psa", 0), ("psb", 0), ("psc", 0), ("psc", 128)), (("psd", 0), ("psd", 128), ("psd", 256), ("psd", 384)),
+             (("pd0", 0), ("pd1", 0), ("pd2", 0), ("pd3", 0)))
+    N1A, N1C, N2A, N2C, NP = 0, 16, 32, 48, 64
+    O0, O1, OP = T.ofa[:, 0:2], T.ofa[:, 2:3], T.ofa[:, 4:7]
+
+    def scores(k, tok, c0, bk, *deps):
+        if k == 2:
+            return [mm(T["pd%d" % h][:, 0:128], tok, c0, c0 + 128, bk, 128 * h, 128 * h + 128, True, True, *deps) for h in range(4)]
+        if k == 1:
+            return [mm(T.psd[:, 0:512], tok, c0, c0 + 128, bk, 0, 512, True, True, *deps)] * 4
+        m = [mm(T[("psa", "psb")[h]][:, 0:128], tok, c0, c0 + 128, bk, 128 * h, 128 * h + 128, True, True, *deps) for h in range(2)]
+        return m + [mm(T.psc[:, 0:256], tok, c0, c0 + 128, bk, 256, 512, True, True)] * 2
+
+    def word(k, h, m, rm, jk, at):
+        s = min(k, 1)
+        e = 512 * s + 128 * h
+        b, o = where[k][h]
+        cv = scan(rm[:, e:e + 128], T.zz[:, 0:128], T[b][:, o:o + 128], m[h])
+        need("s", cv, c_f)
+        return cv, done("s", SC.activation(jk[:, e:e + 128], rm[:, e:e + 128], F.Sign, bias=rm[:, e + 127:e + 128], scale=-1.0,
+                                           accum_out=T.nf[:, at + 4 * s + h:at + 4 * s + h + 1]))
+
+    def part_hi(at, off, xt, n, *deps):
+        need("v", *deps)
+        return done("v", V.tensor_scalar(T[xt][:, 0:n], T.nf[:, at:at + 16].indirect(off), RND, RND, A.add, A.subtract))
+
+    def part_lo(at, off, xt, n, c):
+        need("v", c)
+        return done("v", V.tensor_tensor(T[xt][:, n:2 * n], T.nf[:, at:at + 16].indirect(off), T[xt][:, 0:n], A.subtract))
+
+    def part_q(xt, c):
+        return quant(T[xt + "q"][:], T[xt + "qs"][:], T[xt][:], c)
+
+    def tolist(bank, xt, w, *deps):
+        mm(bank[:, 0:128], "wlq", 0, 128, xt + "q", 0, 128, True, False, *deps)
+        return mm(bank[:, 0:128], "wlq", 0, 128, xt + "q", w, 128 + w, False, True)
+
+    def book2(h, *deps):
+        return quant(T.b2q[:, 128 * h:128 * h + 128], T.b2qs[:, 128 * h:128 * h + 128], T.bm2[:, 512 * h:512 * h + 512], *deps)
+
+    def unpack(b):
+        return mm(T["pd%d" % b][:, 0:192], "epq", 128 * b, 128 * b + 128, "zq", 0, 192, True, True, c_db[b])
+
+    ma = scores(0, "zq", 0, "b1q", ("zin", 2 * landing), zo[0], zo[1], c_b1)
+    mc = scores(1, "zq", 64, "b1q")
+    md = [unpack(b) for b in range(4)]
+    word(0, 0, ma, T.rm1, T.jk1, N1A)
+    cq1 = ts(T.q1[:], T.ai[:], 48.0, -192.0, A.mult, A.add, c_bi)
+    word(0, 1, ma, T.rm1, T.jk1, N1A)
+    ts(T.tf[:], T.bi[:], 48.0, None, A.is_lt, None)
+    cq1 = tt(T.q1[:], T.q1[:], T.bi[:], A.add, cq1)
+    word(0, 2, ma, T.rm1, T.jk1, N1A)
+    c_pf = tt(T.nf[:, 64:72:4], T.q1[:], T.tf[:], A.mult, cq1, c_f)
+    _, sa = word(0, 3, ma, T.rm1, T.jk1, N1A)
+    cx = part_hi(NP, OP, "xp", 48, c_pf, c_xp, ("oin", landing), ("do", 16))
+    word(1, 0, mc, T.rm1, T.jk1, N1C)
+    cx = part_lo(NP, OP, "xp", 48, cx)
+    word(1, 1, mc, T.rm1, T.jk1, N1C)
+    c = part_hi(N1A, O0, "xa", 32, sa, c_xa)
+    word(1, 2, mc, T.rm1, T.jk1, N1C)
+    c = part_lo(N1A, O0, "xa", 32, c)
+    _, sc = word(1, 3, mc, T.rm1, T.jk1, N1C)
+    c = part_q("xa", c)
+    la = tolist(T.psa, "xa", 8, c, c_w)
+    cx = part_q("xp", cx)
+    c = part_hi(N1C, O1, "xc", 16, sc, c_xc)
+    book2(2, c_m2)
+    c = part_lo(N1C, O1, "xc", 16, c)
+    book2(3)
+    c = part_q("xc", c)
+    lc = tolist(T.psb, "xc", 4, c)
+    mp = tolist(T.psd, "xp", 12, cx)
+    c_d = [act(T.dq[:, 192 * b:192 * b + 192], T["pd%d" % b][:, 0:192], F.Copy, md[b]) for b in range(2)]
+
+    def rest_gather(d0, d1, lst, c):
+        need("v", c)
+        for b in range(2):
+            need("v", c_d[b])
+            done("v", V.tensor_tensor(T.rt[:, 4 * d0 + b:4 * d1:4], T.db[:, 128 * b:128 * b + 128].indirect(lst), T.dq[:, 192 * b + d0:192 * b + d1], A.add))
+        return [act(T["g%d" % b][:, d0:d1], T.db[:, 128 * b:128 * b + 128].indirect(lst), F.Copy, c) for b in (2, 3)]
+
+    def rest_add(d0, d1, cg):
+        for b in (2, 3):
+            c = tt(T.rt[:, 4 * d0 + b:4 * d1:4], T["g%d" % b][:, d0:d1], T["pd%d" % b][:, d0:d1], A.add, cg[b - 2], md[b])
+        return c
+    c_l = copy(T.l1[:, 0:8], T.psa[:, 0:8], la)
+    cg = rest_gather(0, 128, T.l1[:, 0:8], c_l)
+    c_l = copy(T.l1[:, 8:12], T.psb[:, 0:4], lc)
+    book2(0, ("db2", 32))
+    c = rest_add(0, 128, cg)
+    c_r = quant(T.raq[:], T.raqs[:], T.rt[:, 0:512], c)
+    c_b2 = book2(1)
+    cg = rest_gather(128, 192, T.l1[:, 8:12], c_l)
+    c_pl = ts(T.pl[:], T.psd[:, 0:12], 192.0, None, A.add, None, mp)
+    c = rest_add(128, 192, cg)
+    c_r2 = quant(T.rcq[:], T.rcqs[:], T.rt[:, 256:768], c)
+    ma = scores(0, "raq", 0, "b2q", c_r, c_l, c_b2)
+    mc = scores(2, "rcq", 0, "b2q", c_r2)
+
+    def part_v(k):
+        return pick_codes("vbq", 64 * k, 64 * k + 64, "p1q", 128, T.l1[:, 4 * k:4 * k + 4])
+    for k in range(3):
+        vs = pick_scales("vbq", 64 * k, 64 * k + 64, "p1q", 128, T.l1[:, 4 * k:4 * k + 4])
+    fan_scales("vbq", "lvq", "vin", vs)
+    act(T.nbf[:, 0:4], T.nf[:, 0:4], F.Copy)
+    act(T.nbf[:, 8:12], T.nf[:, 20:24], F.Copy)
+    for h in range(4):
+        _, sa = word(0, h, ma, T.rm2, T.jk2, N2A)
+    for h in range(3):
+        word(2, h, mc, T.rm2, T.jk2, N2C)
+    c = part_hi(N2A, O0, "xa", 32, sa)
+    vc, sc = word(2, 3, mc, T.rm2, T.jk2, N2C)
+    c = part_lo(N2A, O0, "xa", 32, c)
+    part_v(0)
+    c = part_q("xa", c)
+    la = tolist(T.psa, "xa", 8, c)
+    c = part_hi(N2C, O1, "xc", 16, sc)
+    part_v(1)
+    c = part_lo(N2C, O1, "xc", 16, c)
+    vv = part_v(2)
+    c = part_q("xc", c)
+    lc = tolist(T.psb, "xc", 4, c)
+    fan_codes("vbq", "lvq", "vin", vv)
+    need("y", vv, vs)
+    dma("y", T.lvq[:, 144:192].bitcast(dt.uint8), T.vbq[:, 144:192].bitcast(dt.uint8), "dv")
+    dma("y", T.lvqs[:, 144:192], T.vbqs[:, 144:192], "dv")
+    act(T.nbf[:, 4:8], T.nf[:, 32:36], F.Copy, sc)
+    c_nb = act(T.nbf[:, 12:16], T.nf[:, 52:56], F.Copy)
+    fan([T.nbf[:, 8 * (a // 2):8 * (a // 2) + 8] for a in range(3)], [T.ln[:, 32 * (2 - a):32 * (2 - a) + 8] for a in range(3)], "nin", c_nb)
+    c_l = ts(T.l2[:, 0:8], T.psa[:, 0:8], T.hcol[:], None, A.add, None, la, c_hcol)
+    pick("v2q", 0, 128, "b2q", 512, T.l2[:, 0:8], c_l)
+    c_l = ts(T.l2[:, 8:9], T.psb[:, 0:1], T.hcol[:], None, A.add, None, lc)
+    c_l2 = ts(T.l2b[:, 0:3], T.psb[:, 1:4], T.hcol[:], None, A.add, None)
+    wv, ws = pick("v2q", 128, 144, "b2q", 512, T.l2[:, 8:9], c_l)
+    fan_codes("v2q", "lwq", "win", wv)
+    fan_scales("v2q", "lwq", "win", ws)
+    wo = pick("lwq", 144, 192, "b2q", 512, T.l2b[:, 0:3], c_l2)
+    c_ln3 = act(T.ln[:, 96:104], T.nbf[:, 8:16], F.Copy, c_nb, c_ln)
+
+    c_q = quant(T.wq[:], T.wqs[:], T.wb[:], ("dw", 16))
+    c_wt = fill(T.wt[:], -1.0)
+    ov, os_ = pick("o1q", 0, 192, "lvq", 208, T.pl[:, 0:12], c_pl, ("vin", 2 * landing), ("dv", 32), ("dz", 64))
+    need("y", ov, os_)
+    dma("y", T.oc[:, 0:768], T.o1q[:].bitcast(dt.uint8), "st")
+    for k in range(4):
+        dma("y", T.osc[4 * k:4 * k + 4, 0:192], T.o1qs[32 * k:32 * k + 4, :], "st")
+    mm(T.psc[:, 0:192], "wq", 0, 128, "o1q", 0, 192, True, False, c_q, ov, os_, vc)
+    need("v", c_ln3, ("nin", landing))
+    c = done("v", V.transpose(T.tr[:], T.ln[:]))
+    c_t = []
+    for k, (a, q, i, n, o) in enumerate(((0, 1, 0, 32, 0), (0, 2, 0, 16, 32), (1, 1, 16, 16, 0), (1, 2, 0, 32, 16),
+                                         (2, 0, 0, 32, 0), (2, 1, 0, 16, 32), (3, 2, 16, 16, 0), (3, 3, 0, 32, 16))):
+        out, in_ = T.wt[0:32, 48 * a + o:48 * a + o + n], T.tr[32 * q:32 * q + 32, 32 * a + i:32 * a + i + n]
+        c_t.append(act(out, in_, F.Copy, c, c_wt) if k % 2 else copy(out, in_, c, c_wt))
+    ov, os_ = pick("o2q", 0, 192, "lwq", 208, T.pl[:, 0:12], ("win", 2 * landing), wo[0], wo[1])
+    m = mm(T.psc[:, 0:192], "wq", 0, 128, "o2q", 0, 192, False, True, ov, os_)
+    need("y", ov)
+    dma("y", T.oc[:, 768:1536], T.o2q[:].bitcast(dt.uint8), "st")
+    need("s", os_)
+    for k in range(4):
+        dma("s", T.osc[4 * k:4 * k + 4, 192:384], T.o2qs[32 * k:32 * k + 4, :], "st")
+    need("v", *c_t)
+    c_n = done("v", V.tensor_copy(T.wno[:], T.wt[:, 0:208].indirect(T.pl[:, 0:12])))
+    c = copy(T.ysb[:], T.psc[:, 0:192], m)
+    need("y", c_n)
+    dma("y", T.wn[:], T.wno[0:8, :], "st")
+    need("y", c)
+    dma("y", T.y[:], T.ysb[:], "st")
+
+    need("y", *[(qsem[q], cnt[q]) for q in cnt])
+    need("y", ("st", 16 * stores[0]))
+    need("g", ("left", left[0]))

@@ -4,16 +4,9 @@ from concourse.mybir import dt, AluOpType, AxisListType, ActivationFunctionType
 A = AluOpType
 F = ActivationFunctionType
 NR = 4
+OT = 896
 LOW = -1e29
 RND = 1.5 * 2.0 ** 27
-
-
-def _codes(n):
-    return ("sbuf", [128, n], "float8_e4m3fn_x4")
-
-
-def _plane(n):
-    return ("sbuf", [128, n], "uint8")
 
 
 def _sb(n, d):
@@ -21,39 +14,40 @@ def _sb(n, d):
 
 
 SCRATCH = {}
-for _n, _w in (("xq", 192), ("cq", 134), ("wq", 128), ("p1q", 128), ("b1q", 512), ("b2q", 512), ("trq", 256), ("wlq", 128), ("epq", 512),
-               ("otq", 134), ("abq", 140), ("xaq", 136), ("xcq", 132), ("xpq", 140), ("zsq", 144), ("zq", 192), ("vbq", 192), ("lvq", 208),
-               ("v2q", 144), ("lwq", 208), ("raq", 128), ("rcq", 128), ("o1q", 192), ("o2q", 192)):
-    SCRATCH[_n] = _codes(_w)
-    SCRATCH[_n + "s"] = _plane(_w)
-for _n, _w in (("xb", 768), ("cb", 536), ("wb", 512), ("pb1", 512), ("pb2", 512), ("bm1", 2048), ("bm2", 2048), ("trb", 516), ("wlb", 512),
-               ("epb", 516), ("ot", 536), ("ab", 560), ("xa", 544), ("xc", 528), ("xp", 560), ("rt", 768), ("zz", 536), ("on1", 128),
+for _n, _w in (("xq", 224), ("wq", 128), ("p1q", 128), ("b1q", 512), ("b2q", 512), ("trq", 256), ("wlq", 128), ("epq", 512),
+               ("otq", 134), ("abq", 140), ("xaq", 136), ("xcq", 132), ("xpq", 140), ("zsq", 144), ("zq", 192), ("vbq", 144), ("lvq", 208),
+               ("v2q", 144), ("lwq", 208), ("raq", 128), ("rcq", 192), ("o1q", 192), ("o2q", 192)):
+    SCRATCH[_n] = _sb(_w, "float8_e4m3fn_x4")
+    SCRATCH[_n + "s"] = _sb(_w, "uint8")
+for _n, _w in (("cx", 976), ("wb", 512), ("pp", 608), ("bm1", 2048), ("trb", 516), ("wlb", 512),
+               ("epb", 516), ("ab", 656), ("rt", 1280), ("zz", 536), ("on1", 128),
                ("t1", 128), ("im", 128), ("jk1", 1024), ("jk2", 1024), ("nbf", 16), ("ln", 128), ("tr", 128)):
     SCRATCH[_n] = _sb(_w, "bfloat16")
-for _n, _w in (("rst", 10), ("rma", 10), ("ua", 11), ("rr", 10), ("hc", 2), ("nl", 2), ("tk", 4), ("tkn", 2), ("ib", 12), ("abx", 12),
+for _n, _w in (("rst", 10), ("rma", 10), ("ua", 11), ("rr", 10), ("hc", 2), ("nl", 2), ("tk", 4), ("ib", 12), ("f0", 1), ("f1", 1),
                ("vl", 1), ("mk", 4), ("hcol", 1), ("df", 1), ("e0", 1), ("e4", 1), ("off", 2), ("rm1", 1024), ("rm2", 1024), ("nf", 80),
                ("tf", 2), ("q1", 2), ("wt", 208), ("wno", 192), ("ysb", 192), ("db", 512), ("dq", 384), ("g2", 192), ("g3", 192)):
     SCRATCH[_n] = _sb(_w, "float32")
-for _n, _w in (("pi", 1), ("pa", 1), ("pb", 1), ("gi", 1), ("ui", 1), ("ti", 1), ("hi", 1), ("vi", 2), ("ai", 2), ("bi", 2)):
+for _n, _w in (("pi", 1), ("pa", 1), ("pb", 1), ("gi", 1), ("ui", 1), ("ti", 1), ("hi", 1), ("vi", 2), ("ai", 2), ("bi", 2), ("t0", 1), ("t2", 1)):
     SCRATCH[_n] = _sb(_w, "int32")
-for _n, _w in (("zl", 12), ("zl2", 4), ("pl", 12), ("l1", 12), ("l2", 12), ("l2b", 4), ("ofo", 2), ("ofa", 8)):
+for _n, _w in (("zl", 12), ("zl2", 4), ("pl", 12), ("l1", 12), ("l1b", 4), ("l2", 12), ("l2b", 4), ("ofo", 2), ("ofa", 8), ("o2", 2)):
     SCRATCH[_n] = _sb(_w, "uint16")
 for _n in ("psa", "psb", "psc", "psd", "pd0", "pd1", "pd2", "pd3"):
     SCRATCH[_n] = ("psum", [128, 512], "float32")
-SEMAPHORES = ["qv", "qs", "qt", "qg", "dx", "dco", "dp1", "dp2", "db2", "dep", "dw", "dz", "dv", "do", "st", "zin", "vin", "win", "nin", "oin",
-              "left"]
+SEMAPHORES = ["qv", "qs", "qt", "qg", "dx", "dco", "dp1", "db2", "dw", "dz", "do", "st", "zin", "vin", "win", "nin", "oin", "left"]
 
 
-def _mask(topo, src, peers):
-    out, far, near = {}, 0, 0
-    for c in peers:
+def _mask(topo, src, peers, kind, who):
+    out, far = {}, 0
+    for k, a in enumerate(who):
+        c = peers[a]
         e = topo.engines(src, c)
-        if topo.die(src) != topo.die(c):
-            out[c] = e[far * 8:far * 8 + 8:2]
+        if len(who) < 3:
+            out[c] = e[k::len(who)]
+        elif topo.die(src) != topo.die(c):
+            out[c] = e[far * 8 + kind:far * 8 + 8:2]
             far += 1
         else:
-            out[c] = e[1 + near * 8:9 + near * 8:2]
-            near += 1
+            out[c] = e[1 - kind::2]
     return out
 
 
@@ -112,69 +106,86 @@ def rank_program(g, core, T, topo):
         need("s", *deps)
         return done("s", SC.activation(out, in_, func))
 
+    def iota(out, pattern, base):
+        return done("g", g.iota(out, pattern, base, 0, allow_small_or_imprecise_dtypes=True))
+
     def mm(out, name, c0, c1, mov, m0, m1, start, stop, *deps):
         need("t", *deps)
         return done("t", TE.matmul_mx(out, T[name][:, c0:c1], T[name + "s"][:, c0:c1], T[mov][:, m0:m1], T[mov + "s"][:, m0:m1], start, stop))
 
-    def pick_codes(dst, d0, d1, win, w1, lst, *deps):
+    def pick_codes(dst, d0, d1, win, w, lst, *deps):
         need("v", *deps)
-        return done("v", V.tensor_copy(T[dst][:, d0:d1].bitcast(dt.uint32), T[win][:, 0:w1].bitcast(dt.uint32).indirect(lst)))
+        return done("v", V.tensor_copy(T[dst][:, d0:d1].bitcast(dt.uint32), T[win][:, w[0]:w[1]].bitcast(dt.uint32).indirect(lst)))
 
-    def pick_scales(dst, d0, d1, win, w1, lst, *deps):
-        return act(T[dst + "s"][:, d0:d1], T[win + "s"][:, 0:w1].indirect(lst), F.Copy, *deps)
+    def pick_scales(dst, d0, d1, win, w, lst, *deps):
+        return act(T[dst + "s"][:, d0:d1], T[win + "s"][:, w[0]:w[1]].indirect(lst), F.Copy, *deps)
 
     def pick(*a):
         return pick_codes(*a), pick_scales(*a)
 
-    peers = [T.cores[(rank + 1 + a) % NR] for a in range(3)]
-    emask = _mask(topo, core, peers)
-    landing = sum(len(_mask(topo, c, [T.cores[(T.rank_of(c) + 1 + a) % NR] for a in range(3)])[core]) for c in peers)
+    ALL = (0, 1, 2)
+    peers = [T.cores[(rank + 1 + a) % NR] for a in ALL]
+
+    def lands(*whos):
+        n = 0
+        for c in peers:
+            for who in whos:
+                n += len(_mask(topo, c, [T.cores[(T.rank_of(c) + 1 + a) % NR] for a in ALL], 0, who).get(core, ()))
+        return n
+    landing = lands(ALL)
     left = [0]
 
-    def fan(srcs, dsts, sem, *deps):
+    def fan(srcs, dsts, sem, *deps, kind=0, who=ALL):
         need("g", *deps)
+        emask = _mask(topo, core, peers, kind, who)
         tr = []
-        for a, c in enumerate(peers):
+        for a in who:
+            c = peers[a]
             rid, pid, _ = topo.addr(c)
             tr.append(RemoteDMATransfer(dst_ids=[DstId(rid=rid, pnc=pid)], dma_engine_mask=sum(1 << e for e in emask[c]),
                                         remote_sem=S[sem], srcs=[srcs[a]], dsts=[dsts[a]]))
             left[0] += len(emask[c])
         g.remote_dma_fused(tr, local_sem=S["left"])
 
-    def fan_codes(src, dst, sem, *c):
-        fan([T[src][:, 48 * a:48 * a + 48].bitcast(dt.uint8) for a in range(3)],
-            [T[dst][:, 48 * (2 - a):48 * (2 - a) + 48].bitcast(dt.uint8) for a in range(3)], sem, *c)
+    def fan_codes(src, dst, sem, *c, who=ALL):
+        fan([T[src][:, 48 * a:48 * a + 48].bitcast(dt.uint8) for a in ALL],
+            [T[dst][:, 48 * (2 - a):48 * (2 - a) + 48].bitcast(dt.uint8) for a in ALL], sem, *c, who=who)
 
-    def fan_scales(src, dst, sem, *c):
-        fan([T[src + "s"][:, 48 * a:48 * a + 48] for a in range(3)], [T[dst + "s"][:, 48 * (2 - a):48 * (2 - a) + 48] for a in range(3)], sem, *c)
+    def fan_scales(src, dst, sem, *c, who=ALL):
+        fan([T[src + "s"][:, 48 * a:48 * a + 48] for a in ALL], [T[dst + "s"][:, 48 * (2 - a):48 * (2 - a) + 48] for a in ALL], sem, *c,
+            kind=1, who=who)
 
-    dma("y", T.xb[:], T.x[:], "dx")
-    dma("s", T.cb[:, 24:40], T.co[:, 0:4 * NR], "dco")
-    dma("y", T.pb1[:], T.b1[:], "dp1")
+    dma("y", T.cx[:, 128:OT], T.x[:], "dx")
+    dma("s", T.cx[:, 24:40], T.co[:, 0:4 * NR], "dco")
+    dma("y", T.pp[:, 64:576], T.b1[:], "dp1")
 
     c_pi = done("g", g.iota(T.pi[:], [[0, 1]], 0, 1))
     c_on = fill(T.on1[:], 1.0)
     c_zz = fill(T.zz[:], 0.0)
-    need("y", c_zz)
-    dma("y", T.epb[:], T.zz[:, 0:516], "dep")
-    dma("y", T.pb2[:], T.b2[:], "dp2")
     need("s", c_zz)
     c_tr = done("s", SC.activation(T.trb[:], T.zz[:, 0:516], F.Identity, bias=1.0))
-    c_ot = act(T.ot[:], T.zz[:], F.Copy)
+    c_ua = act(T.ua[:], T.zz[:, 0:11], F.Copy)
+    c_e0 = act(T.epb[:], T.zz[:, 0:516], F.Copy)
+    c_w0 = act(T.wlb[:], T.zz[:, 0:512], F.Copy)
+    c_ln = act(T.ln[:], T.zz[:, 0:128], F.Copy)
     need("g", c_on)
     c_t1 = done("g", g.affine_select(T.t1[:], T.on1[:], [[1, 128]], A.is_gt, 0.0, 0, -1))
-    c_cb = done("g", g.iota(T.cb[:, 40:536], [[0, 496]], 0, 0, allow_small_or_imprecise_dtypes=True))
+    if rank < NR - 1:
+        iota(T.ib[:, 0:9 - 3 * rank], [[256, 3 - rank], [16, 3]], 1280 + 256 * rank)
+    c_ib = iota(T.ib[:, 9 - 3 * rank:12], [[256, rank + 1], [16, 3]], 1024)
+    c_im = iota(T.im[:], [[0, 8], [1, 16]], 0)
     ts(T.gi[:], T.pi[:], 4, None, A.arith_shift_right, None, c_pi)
     c = ts(T.ui[:], T.pi[:], 2, 3, A.arith_shift_right, A.bitwise_and)
     ts(T.ti[:], T.pi[:], 3 if rank < 2 else 0, None, A.bitwise_and, None)
     c_hi = ts(T.hi[:], T.pi[:], 5, None, A.arith_shift_right, None)
     c = tt(T.df[:], T.gi[:], T.ui[:], A.subtract, c)
-    c_cb0 = fill(T.cb[:, 0:24], 0.0)
-    for h in range(4):
-        c_mk = ts(T.mk[:, h:h + 1], T.hi[:], float(h), None, A.is_equal, None, c_hi)
+    fill(T.cx[:, 0:24], 0.0)
+    c_hcol = ts(T.hcol[:], T.hi[:], 128.0, None, A.mult, None, c_hi)
     if rank % 2 == 0:
         ts(T.e0[:], T.df[:], 0.0, None, A.is_equal, None, c)
     c = ts(T.e4[:], T.df[:], 4.0, None, A.is_equal, None, c)
+    c_cb = fill(T.cx[:, 40:128], 0.0)
+    c_ot = fill(T.cx[:, OT:OT + 80], 0.0)
     c_tr = fill(T.trb[:, 2:516:4], 0.0, c_tr)
     for k, (e, v) in enumerate((((T.e0, -8.0), (T.e4, -8.0)), ((T.e4, -4.0),))[rank % 2]):
         c = ts(T.off[:, k:k + 1], T.ti[:], v, e[:], A.add, A.mult, c)
@@ -182,40 +193,31 @@ def rank_program(g, core, T, topo):
     c_rs = fill(T.rst[:], 0.0)
     c_of = ts(T.ofo[:, 0:wide], T.off[:, 0:wide], 8.0, None, A.add, None, c)
     c_rs = fill(T.rst[:, 4:7], LOW, c_rs)
+    c_mk = ts(T.mk[:], T.im[:, 0:4], 128.0, T.hcol[:], A.mult, A.is_equal, c_im, c_hcol)
     need("g", c_t1, c_tr)
     c_tri = done("g", g.affine_select(T.trb[:, 1:513:4], T.t1[:], [[1, 128]], A.not_equal, 1024.0, 0, -1))
     need("g", c_ot)
-    c_oi = done("g", g.iota(T.ot[:, 27:75:4], [[0, 2], [2, 6]], 0, 0, allow_small_or_imprecise_dtypes=True))
+    c_oi = iota(T.cx[:, OT + 27:OT + 75:4], [[0, 2], [2, 6]], 0)
     own = slice(2 * rank, 2 * rank + wide)
     fan([T.ofo[:, 0:wide]] * 3, [T.ofa[:, own]] * 3, "oin", c_of)
     need("y", c_of)
     dma("y", T.ofa[:, own], T.ofo[:, 0:wide], "do")
-    if rank < NR - 1:
-        done("g", g.iota(T.ib[:, 0:9 - 3 * rank], [[256, 3 - rank], [16, 3]], 1280 + 256 * rank, 0, allow_small_or_imprecise_dtypes=True))
-    c_ib = done("g", g.iota(T.ib[:, 9 - 3 * rank:12], [[256, rank + 1], [16, 3]], 1024, 0, allow_small_or_imprecise_dtypes=True))
-    c_im = done("g", g.iota(T.im[:], [[0, 8], [1, 16]], 0, 0, allow_small_or_imprecise_dtypes=True))
-    need("g", ("dep", 16))
+    need("g", c_e0)
     c_ep = done("g", g.affine_select(T.epb[:, 4:516:4], T.on1[:], [[1, 128]], A.is_equal, 0.0, 0, -1))
-    c_w0 = act(T.wlb[:], T.zz[:, 0:512], F.Copy)
-    c_xp = act(T.xp[:, 96:560], T.zz[:, 0:464], F.Copy)
 
-    def masked(bm, pb, h):
-        return done("s", SC.activation(bm[:, 512 * h:512 * h + 512], pb[:], F.Copy, scale=T.mk[:, h:h + 1]))
     need("s", c_mk, ("dp1", 16))
-    for h in range(3):
-        masked(T.bm1, T.pb1, h)
+    for h in range(4):
+        c_m1 = done("s", SC.activation(T.bm1[:, 512 * h:512 * h + 512], T.pp[:, 64:576], F.Copy, scale=T.mk[:, h:h + 1]))
 
-    c_q = quant(T.cq[:], T.cqs[:], T.cb[:], ("dco", 16), c_cb, c_cb0)
-    c_x = quant(T.xq[:], T.xqs[:], T.xb[:], ("dx", 16))
-    need("y", c_q)
+    c_x = quant(T.xq[:], T.xqs[:], T.cx[:, 0:OT], ("dco", 16), c_cb, ("dx", 16))
+    need("y", c_x)
     for b in ("lvq", "lwq"):
-        dma("y", T[b][:, 192:208].bitcast(dt.uint8), T.cq[:, 64:80].bitcast(dt.uint8), "dz")
-        dma("y", T[b + "s"][:, 192:208], T.cqs[:, 64:80], "dz")
-    mm(T.psa[:, 0:128], "xq", 0, 128, "cq", 6, 134, True, False, c_x)
-    m = mm(T.psa[:, 0:128], "xq", 64, 192, "cq", 0, 128, False, True)
-    c_ua = fill(T.ua[:], 0.0)
+        dma("y", T[b][:, 192:208].bitcast(dt.uint8), T.xq[:, 16:32].bitcast(dt.uint8), "dz")
+        dma("y", T[b + "s"][:, 192:208], T.xqs[:, 16:32], "dz")
+    mm(T.psa[:, 0:128], "xq", 32, 160, "xq", 6, 134, True, False, c_x)
+    m = mm(T.psa[:, 0:128], "xq", 96, 224, "xq", 0, 128, False, True)
     c_vl = ts(T.vl[:], T.pi[:], 64.0, None, A.is_ge, None)
-    c_o1 = fill(T.ot[:, 1:64:4], -7.5 / 128, c_ot)
+    c_o1 = fill(T.cx[:, OT + 1:OT + 64:4], -7.5 / 128, c_ot)
     for k in range(2):
         quant(T.trq[:, 128 * k:128 * k + 128], T.trqs[:, 128 * k:128 * k + 128], T.trb[:, 1 + 2 * k:513 + 2 * k], c_tri)
 
@@ -227,50 +229,44 @@ def rank_program(g, core, T, topo):
     u = ts(T.ua[:, 1:5], T.rma[:, 0:4], T.rma[:, 3:4], None, A.is_equal, None, s, c_ua)
     u = ts(T.ua[:, 7:11], T.rma[:, 6:10], T.rma[:, 9:10], T.vl[:], A.is_equal, A.mult, c_vl)
     c_pb = ts(T.pb[:], T.pi[:], 15, None, A.bitwise_and, None)
-    o = tt(T.ot[:, 24:64:4], T.ua[:, 1:11], T.ua[:, 0:10], A.subtract, u, c_o1)
-    c_o = quant(T.otq[:], T.otqs[:], T.ot[:], o, c_oi)
+    o = tt(T.cx[:, OT + 24:OT + 64:4], T.ua[:, 1:11], T.ua[:, 0:10], A.subtract, u, c_o1)
+    c_o = quant(T.otq[:], T.otqs[:], T.cx[:, OT + 64 - 536:OT + 64], o, c_oi)
     mm(T.psc[:, 0:128], "trq", 0, 128, "otq", 6, 134, True, False, c_o)
     m = mm(T.psc[:, 0:128], "trq", 128, 256, "otq", 0, 128, False, True)
     ts(T.tk[:, 2:3], T.pa[:], 64.0, T.vl[:], A.add, A.mult, c_pb)
-    c = ts(T.tk[:, 3:4], T.pb[:], T.vl[:], None, A.mult, None)
+    ts(T.tk[:, 3:4], T.pb[:], T.vl[:], None, A.mult, None)
     copy(T.tk[:, 0:1], T.pa[:])
     c_tk = copy(T.tk[:, 1:2], T.pb[:])
-    c_tn = ts(T.tkn[:], T.tk[:, 2:4], -0.0625, None, A.mult, None, c)
-    c_ln = fill(T.ln[:], 0.0)
-    r = scan(T.rr[:], T.rst[:], T.psc[:, 0:10], m)
+    ts(T.t0[:], T.pi[:], 1, None, A.bitwise_and, None)
+    ct = ts(T.t2[:], T.pi[:], 1, 1, A.arith_shift_right, A.bitwise_and)
+    r = scan(T.rr[:], T.rst[:], T.psc[:, 118:128], m)
     c_hc = ts(T.hc[:], T.rr[:, 3:10:6], RND, RND, A.add, A.subtract, r)
-    need("s", c_hc, c_ib, c_tn)
-    c = done("s", SC.activation(T.abx[:], T.ib[:], F.Abs, bias=T.hc[:, 1:2], scale=-1.0))
-    need("s", c)
-    for t in (2, 3):
-        c_b = done("s", SC.activation(T.ab[:, 512 + t:560:4], T.abx[:], F.Relu, bias=T.tk[:, t:t + 1], scale=T.tkn[:, t - 2:t - 1]))
-    c_m1 = masked(T.bm1, T.pb1, 3)
     c_nl = tt(T.nl[:], T.hc[:], T.rr[:, 3:10:6], A.subtract, c_hc)
-    for t in range(2):
-        ts(T.ab[:, 512 + t:560:4], T.ib[:], T.hc[:, 0:1], T.tk[:, t:t + 1], A.is_equal, A.mult, c_tk, c_ib)
     for t in range(4):
-        c_a = ts(T.ab[:, t:512:4], T.im[:], T.nl[:, t // 2:t // 2 + 1], 7.5, A.subtract, A.is_equal, c_nl, c_im) if False else \
-            ts(T.ab[:, t:512:4], T.im[:], T.nl[:, t // 2:t // 2 + 1], 7.5, A.add, A.is_equal, c_nl, c_im)
-    c_a = quant(T.abq[:], T.abqs[:], T.ab[:], c_a, c_b)
+        ts(T.ab[:, 512 + t:560:4], T.ib[:], T.hc[:, t // 2:t // 2 + 1], T.tk[:, t:t + 1], A.is_equal, A.mult, c_tk, c_ib)
+    for t in range(4):
+        c_a = ts(T.ab[:, t:512:4], T.im[:], T.nl[:, t // 2:t // 2 + 1], 7.5, A.add, A.is_equal, c_nl, c_im)
+    c_a = quant(T.abq[:], T.abqs[:], T.ab[:, 0:560], c_a)
     m0 = mm(T.psa[:, 0:128], "abq", 0, 128, "abq", 12, 140, True, True, c_a)
 
     def e_tile(b):
         return quant(T.epq[:, 128 * b:128 * b + 128], T.epqs[:, 128 * b:128 * b + 128], T.epb[:, 4 - b:516 - b], c_ep)
     c_e = [e_tile(0), e_tile(1)]
     c_l = copy(T.zl[:, 0:9], T.psa[:, 116:125], m0)
-    zv, zs = pick("zsq", 0, 144, "xq", 192, T.zl[:, 0:9], c_l)
+    zv, zs = pick("zsq", 0, 144, "xq", (32, 224), T.zl[:, 0:9], c_l)
     fan_codes("zsq", "zq", "zin", zv, c_ln)
     fan_scales("zsq", "zq", "zin", zs)
+    iota(T.rt[:, 512:768], [[0, 256]], 0)
+    c_rz = iota(T.rt[:, 1024:1280], [[0, 256]], 0)
     c_l = copy(T.zl2[:, 0:3], T.psa[:, 125:128])
-    c_p1 = quant(T.p1q[:], T.p1qs[:], T.pb1[:], ("dp1", 16))
-    zo = pick("zq", 144, 192, "xq", 192, T.zl2[:, 0:3], c_l)
+    c_p1 = quant(T.p1q[:], T.p1qs[:], T.pp[:, 64:576], ("dp1", 16))
+    zo = pick("zq", 144, 192, "xq", (32, 224), T.zl2[:, 0:3], c_l)
 
-    c_xc = done("g", g.iota(T.xc[:, 32:528], [[0, 496]], 0, 0, allow_small_or_imprecise_dtypes=True))
-    for h in range(2):
-        c_g = done("g", g.iota(T.bm2[:, 512 * h:512 * h + 512], [[0, 512]], 0, 0, allow_small_or_imprecise_dtypes=True))
-    need("y", c_g)
-    for h in range(2):
-        dma("y", T.bm2[32 * h:32 * h + 32, 512 * h:512 * h + 512], T.b2[32 * h:32 * h + 32, :], "db2")
+    c_b1 = quant(T.b1q[:], T.b1qs[:], T.bm1[:], c_m1)
+    need("y", c_b1)
+    for h in range(4):
+        dma("y", T.bm1[32 * h:32 * h + 32, 512 * h:512 * h + 512], T.b2[32 * h:32 * h + 32, :], "db2")
+    need("y", ("zin", 2 * landing))
     dma("y", T.wb[:], T.w[:], "dw")
     c_db = []
 
@@ -278,34 +274,35 @@ def rank_program(g, core, T, topo):
         m = mm(T["pd%d" % b][:, 0:128], "epq", 128 * b, 128 * b + 128, "p1q", 0, 128, True, True, c_e[b], c_p1)
         need("s", m)
         c_db.append(done("s", SC.activation(T.db[:, 128 * b:128 * b + 128], T["pd%d" % b][:, 0:128], F.Copy, scale=-1.0)))
+    c_f = act(T.nf[:], T.zz[:, 0:80], F.Copy)
     table(0)
     table(1)
-    c_xa = act(T.xa[:, 64:544], T.zz[:, 0:480], F.Copy)
     c_e.append(e_tile(2))
     c_e.append(e_tile(3))
     table(2)
     table(3)
-    c_b1 = quant(T.b1q[:], T.b1qs[:], T.bm1[:], c_m1)
-    need("s", ("dp2", 16))
-    for h in (2, 3):
-        c_m2 = masked(T.bm2, T.pb2, h)
-    c_f = fill(T.nf[:], 0.0)
+    c_wt = done("s", SC.activation(T.wt[:], T.zz[:, 0:208], F.Identity, bias=-1.0))
+
+    def book2(h, *deps):
+        return quant(T.b2q[:, 128 * h:128 * h + 128], T.b2qs[:, 128 * h:128 * h + 128], T.bm1[:, 512 * h:512 * h + 512], *deps)
+    c = ts(T.vi[:], T.rr[:, 3:10:6], -1016.5 + 256 * (3 - rank), None, A.add, None)
+    ct = ts(T.f0[:], T.t0[:], 4.0, T.df[:], A.mult, A.is_equal, ct)
     for t in range(4):
         c_w = ts(T.wlb[:, 129 * t:128 * t + 128:4], T.im[:, 0:32], T.tk[:, 1:2], None, A.is_equal, None, c_w0)
-    c = ts(T.vi[:], T.rr[:, 3:10:6], -1016.5 + 256 * (3 - rank), None, A.add, None)
-    c_w = quant(T.wlq[:], T.wlqs[:], T.wlb[:], c_w)
+    ct = ts(T.f1[:], T.t2[:], -4.0, T.f0[:], A.add, A.mult, ct)
     ts(T.ai[:], T.vi[:], 8, 3, A.arith_shift_right, A.bitwise_and, c)
     c_bi = ts(T.bi[:], T.vi[:], 255, None, A.bitwise_and, None)
-    c_hcol = ts(T.hcol[:], T.hi[:], 128.0, None, A.mult, None)
+    c_w = quant(T.wlq[:], T.wlqs[:], T.wlb[:], c_w)
 
     where = ((("psa", 0), ("psb", 0), ("psc", 0), ("psc", 128)), (("psd", 0), ("psd", 128), ("psd", 256), ("psd", 384)),
-             (("pd0", 0), ("pd1", 0), ("pd2", 0), ("pd3", 0)))
+             (("pd0", 0), ("pd1", 0)))
     N1A, N1C, N2A, N2C, NP = 0, 16, 32, 48, 64
-    O0, O1, OP = T.ofa[:, 0:2], T.ofa[:, 2:3], T.ofa[:, 4:7]
+    O0, O1, OP, O2 = T.ofa[:, 0:2], T.ofa[:, 2:3], T.ofa[:, 4:7], T.o2[:, 0:1]
 
     def scores(k, tok, c0, bk, *deps):
         if k == 2:
-            return [mm(T["pd%d" % h][:, 0:128], tok, c0, c0 + 128, bk, 128 * h, 128 * h + 128, True, True, *deps) for h in range(4)]
+            return [mm(T["pd%d" % (h // 2)][:, 0:128], tok, 64 - 64 * (h % 2), 192 - 64 * (h % 2), bk, 128 * h, 128 * h + 128,
+                       h % 2 == 0, h % 2 == 1, *deps) for h in range(4)][1::2]
         if k == 1:
             return [mm(T.psd[:, 0:512], tok, c0, c0 + 128, bk, 0, 512, True, True, *deps)] * 4
         m = [mm(T[("psa", "psb")[h]][:, 0:128], tok, c0, c0 + 128, bk, 128 * h, 128 * h + 128, True, True, *deps) for h in range(2)]
@@ -320,23 +317,25 @@ def rank_program(g, core, T, topo):
         return cv, done("s", SC.activation(jk[:, e:e + 128], rm[:, e:e + 128], F.Sign, bias=rm[:, e + 127:e + 128], scale=-1.0,
                                            accum_out=T.nf[:, at + 4 * s + h:at + 4 * s + h + 1]))
 
+    XT = {"xa": (T.pp, 0, 0, 544), "xc": (T.pp, 576, 80, 608), "xp": (T.ab, 560, 96, 656)}
+
     def part_hi(at, off, xt, n, *deps):
         need("v", *deps)
-        return done("v", V.tensor_scalar(T[xt][:, 0:n], T.nf[:, at:at + 16].indirect(off), RND, RND, A.add, A.subtract))
+        buf, o = XT[xt][0:2]
+        return done("v", V.tensor_scalar(buf[:, o:o + n], T.nf[:, at:at + 16].indirect(off), RND, RND, A.add, A.subtract))
 
     def part_lo(at, off, xt, n, c):
         need("v", c)
-        return done("v", V.tensor_tensor(T[xt][:, n:2 * n], T.nf[:, at:at + 16].indirect(off), T[xt][:, 0:n], A.subtract))
+        buf, o = XT[xt][0:2]
+        return done("v", V.tensor_tensor(buf[:, o + n:o + 2 * n], T.nf[:, at:at + 16].indirect(off), buf[:, o:o + n], A.subtract))
 
     def part_q(xt, c):
-        return quant(T[xt + "q"][:], T[xt + "qs"][:], T[xt][:], c)
+        buf, _, w0, w1 = XT[xt]
+        return quant(T[xt + "q"][:], T[xt + "qs"][:], buf[:, w0:w1], c)
 
     def tolist(bank, xt, w, *deps):
         mm(bank[:, 0:128], "wlq", 0, 128, xt + "q", 0, 128, True, False, *deps)
         return mm(bank[:, 0:128], "wlq", 0, 128, xt + "q", w, 128 + w, False, True)
-
-    def book2(h, *deps):
-        return quant(T.b2q[:, 128 * h:128 * h + 128], T.b2qs[:, 128 * h:128 * h + 128], T.bm2[:, 512 * h:512 * h + 512], *deps)
 
     def unpack(b):
         return mm(T["pd%d" % b][:, 0:192], "epq", 128 * b, 128 * b + 128, "zq", 0, 192, True, True, c_db[b])
@@ -352,94 +351,100 @@ def rank_program(g, core, T, topo):
     word(0, 2, ma, T.rm1, T.jk1, N1A)
     c_pf = tt(T.nf[:, 64:72:4], T.q1[:], T.tf[:], A.mult, cq1, c_f)
     _, sa = word(0, 3, ma, T.rm1, T.jk1, N1A)
-    cx = part_hi(NP, OP, "xp", 48, c_pf, c_xp, ("oin", landing), ("do", 16))
+    cx = part_hi(NP, OP, "xp", 48, c_pf, ("oin", landing), ("do", 16))
     word(1, 0, mc, T.rm1, T.jk1, N1C)
     cx = part_lo(NP, OP, "xp", 48, cx)
     word(1, 1, mc, T.rm1, T.jk1, N1C)
-    c = part_hi(N1A, O0, "xa", 32, sa, c_xa)
+    book2(0, ("db2", 64))
+    c = part_hi(N1A, O0, "xa", 32, sa)
     word(1, 2, mc, T.rm1, T.jk1, N1C)
     c = part_lo(N1A, O0, "xa", 32, c)
     _, sc = word(1, 3, mc, T.rm1, T.jk1, N1C)
     c = part_q("xa", c)
     la = tolist(T.psa, "xa", 8, c, c_w)
     cx = part_q("xp", cx)
-    c = part_hi(N1C, O1, "xc", 16, sc, c_xc)
-    book2(2, c_m2)
+    book2(1)
+    book2(2)
+    c_d = [act(T.dq[:, 192 * b:192 * b + 192], T["pd%d" % b][:, 0:192], F.Copy, md[b]) for b in range(2)]
+    c = part_hi(N1C, O1, "xc", 16, sc)
+    c_la = copy(T.l1[:, 0:8], T.psa[:, 0:8], la)
     c = part_lo(N1C, O1, "xc", 16, c)
-    book2(3)
+    c_b2 = book2(3)
     c = part_q("xc", c)
     lc = tolist(T.psb, "xc", 4, c)
     mp = tolist(T.psd, "xp", 12, cx)
-    c_d = [act(T.dq[:, 192 * b:192 * b + 192], T["pd%d" % b][:, 0:192], F.Copy, md[b]) for b in range(2)]
 
-    def rest_gather(d0, d1, lst, c):
-        need("v", c)
+    def rest_gather(d0, d1, lst, *c):
+        need("v", *c)
         for b in range(2):
             need("v", c_d[b])
-            done("v", V.tensor_tensor(T.rt[:, 4 * d0 + b:4 * d1:4], T.db[:, 128 * b:128 * b + 128].indirect(lst), T.dq[:, 192 * b + d0:192 * b + d1], A.add))
-        return [act(T["g%d" % b][:, d0:d1], T.db[:, 128 * b:128 * b + 128].indirect(lst), F.Copy, c) for b in (2, 3)]
+            done("v", V.tensor_tensor(T.rt[:, 6 * d0 + b:2 * d0 + 4 * d1:4], T.db[:, 128 * b:128 * b + 128].indirect(lst),
+                                      T.dq[:, 192 * b + d0:192 * b + d1], A.add))
+        return [act(T["g%d" % b][:, d0:d1], T.db[:, 128 * b:128 * b + 128].indirect(lst), F.Copy, c[0]) for b in (2, 3)]
 
     def rest_add(d0, d1, cg):
         for b in (2, 3):
-            c = tt(T.rt[:, 4 * d0 + b:4 * d1:4], T["g%d" % b][:, d0:d1], T["pd%d" % b][:, d0:d1], A.add, cg[b - 2], md[b])
+            c = tt(T.rt[:, 6 * d0 + b:2 * d0 + 4 * d1:4], T["g%d" % b][:, d0:d1], T["pd%d" % b][:, d0:d1], A.add, cg[b - 2], md[b])
         return c
-    c_l = copy(T.l1[:, 0:8], T.psa[:, 0:8], la)
-    cg = rest_gather(0, 128, T.l1[:, 0:8], c_l)
-    c_l = copy(T.l1[:, 8:12], T.psb[:, 0:4], lc)
-    book2(0, ("db2", 32))
-    c = rest_add(0, 128, cg)
-    c_r = quant(T.raq[:], T.raqs[:], T.rt[:, 0:512], c)
-    c_b2 = book2(1)
-    cg = rest_gather(128, 192, T.l1[:, 8:12], c_l)
-    c_pl = ts(T.pl[:], T.psd[:, 0:12], 192.0, None, A.add, None, mp)
-    c = rest_add(128, 192, cg)
-    c_r2 = quant(T.rcq[:], T.rcqs[:], T.rt[:, 256:768], c)
-    ma = scores(0, "raq", 0, "b2q", c_r, c_l, c_b2)
-    mc = scores(2, "rcq", 0, "b2q", c_r2)
 
-    def part_v(k):
-        return pick_codes("vbq", 64 * k, 64 * k + 64, "p1q", 128, T.l1[:, 4 * k:4 * k + 4])
-    for k in range(3):
-        vs = pick_scales("vbq", 64 * k, 64 * k + 64, "p1q", 128, T.l1[:, 4 * k:4 * k + 4])
+    def part_v(k, f):
+        return f("vbq", 64 * k, min(64 * k + 64, 144), "p1q", (0, 128), T.l1[:, 4 * k:min(4 * k + 4, 9)])
+    cg = rest_gather(0, 128, T.l1[:, 0:8], c_la)
+    part_v(0, pick_scales)
+    part_v(1, pick_scales)
+    act(T.nbf[:, 0:4], T.nf[:, 0:4], F.Copy, sc)
+    c_n1 = act(T.nbf[:, 8:16], T.nf[:, 20:28], F.Copy)
+    c_l = copy(T.l1[:, 8:12], T.psb[:, 124:128], lc)
+    c = rest_add(0, 128, cg)
+    c_lb = copy(T.l1b[:, 0:3], T.psb[:, 125:128])
+    c_r = quant(T.raq[:], T.raqs[:], T.rt[:, 0:512], c)
+    ma = scores(0, "raq", 0, "b2q", c_r, c_lb, c_b2)
+    cg = rest_gather(128, 192, T.l1[:, 8:12], c_l, c_rz)
+    vs = part_v(2, pick_scales)
     fan_scales("vbq", "lvq", "vin", vs)
-    act(T.nbf[:, 0:4], T.nf[:, 0:4], F.Copy)
-    act(T.nbf[:, 8:12], T.nf[:, 20:24], F.Copy)
-    for h in range(4):
-        _, sa = word(0, h, ma, T.rm2, T.jk2, N2A)
-    for h in range(3):
-        word(2, h, mc, T.rm2, T.jk2, N2C)
+    word(0, 0, ma, T.rm2, T.jk2, N2A)
+    c = rest_add(128, 192, cg)
+    word(0, 1, ma, T.rm2, T.jk2, N2A)
+    c_r2 = quant(T.rcq[:], T.rcqs[:], T.rt[:, 512:1280], c)
+    mc = scores(2, "rcq", 0, "b2q", c_r2)
+    word(0, 2, ma, T.rm2, T.jk2, N2A)
+    part_v(0, pick_codes)
+    _, sa = word(0, 3, ma, T.rm2, T.jk2, N2A)
+    part_v(1, pick_codes)
+    word(2, 0, mc, T.rm2, T.jk2, N2C)
+    vv = part_v(2, pick_codes)
+    fan_codes("vbq", "lvq", "vin", vv)
+    vc, sc = word(2, 1, mc, T.rm2, T.jk2, N2C)
     c = part_hi(N2A, O0, "xa", 32, sa)
-    vc, sc = word(2, 3, mc, T.rm2, T.jk2, N2C)
+    c_o2 = ts(T.o2[:, 0:1], T.f1[:], 8.0, None, A.add, None, ct)
     c = part_lo(N2A, O0, "xa", 32, c)
-    part_v(0)
     c = part_q("xa", c)
     la = tolist(T.psa, "xa", 8, c)
-    c = part_hi(N2C, O1, "xc", 16, sc)
-    part_v(1)
-    c = part_lo(N2C, O1, "xc", 16, c)
-    vv = part_v(2)
+    c = part_hi(N2C, O2, "xc", 16, sc, c_o2)
+    c_pl = ts(T.pl[:], T.psd[:, 116:128], 192.0, None, A.add, None, mp)
+    c = part_lo(N2C, O2, "xc", 16, c)
     c = part_q("xc", c)
     lc = tolist(T.psb, "xc", 4, c)
-    fan_codes("vbq", "lvq", "vin", vv)
-    need("y", vv, vs)
-    dma("y", T.lvq[:, 144:192].bitcast(dt.uint8), T.vbq[:, 144:192].bitcast(dt.uint8), "dv")
-    dma("y", T.lvqs[:, 144:192], T.vbqs[:, 144:192], "dv")
-    act(T.nbf[:, 4:8], T.nf[:, 32:36], F.Copy, sc)
-    c_nb = act(T.nbf[:, 12:16], T.nf[:, 52:56], F.Copy)
-    fan([T.nbf[:, 8 * (a // 2):8 * (a // 2) + 8] for a in range(3)], [T.ln[:, 32 * (2 - a):32 * (2 - a) + 8] for a in range(3)], "nin", c_nb)
     c_l = ts(T.l2[:, 0:8], T.psa[:, 0:8], T.hcol[:], None, A.add, None, la, c_hcol)
-    pick("v2q", 0, 128, "b2q", 512, T.l2[:, 0:8], c_l)
-    c_l = ts(T.l2[:, 8:9], T.psb[:, 0:1], T.hcol[:], None, A.add, None, lc)
-    c_l2 = ts(T.l2b[:, 0:3], T.psb[:, 1:4], T.hcol[:], None, A.add, None)
-    wv, ws = pick("v2q", 128, 144, "b2q", 512, T.l2[:, 8:9], c_l)
-    fan_codes("v2q", "lwq", "win", wv)
-    fan_scales("v2q", "lwq", "win", ws)
-    wo = pick("lwq", 144, 192, "b2q", 512, T.l2b[:, 0:3], c_l2)
+    act(T.nbf[:, 4:8], T.nf[:, 32:36], F.Copy, sc, c_n1)
+    act(T.nbf[32:64, 12:16], T.nf[96:128, 32:36], F.Copy)
+    act(T.nbf[64:128, 12:16:2], T.nf[0:64, 52:54], F.Copy)
+    c_nb = act(T.nbf[64:128, 13:16:2], T.nf[64:128, 52:54], F.Copy)
+    fan([T.nbf[:, 8 * (a // 2):8 * (a // 2) + 8] for a in ALL], [T.ln[:, 32 * (2 - a):32 * (2 - a) + 8] for a in ALL], "nin", c_nb)
+    wv, ws = pick("v2q", 0, 128, "b2q", (0, 512), T.l2[:, 0:8], c_l)
+    fan_codes("v2q", "lwq", "win", wv, who=(0, 1))
+    fan_scales("v2q", "lwq", "win", ws, who=(0, 1))
+    c_l = ts(T.l2[:, 8:9], T.psb[:, 124:125], T.hcol[:], None, A.add, None, lc)
+    c_l2 = ts(T.l2b[:, 0:3], T.psb[:, 125:128], T.hcol[:], None, A.add, None)
+    wv, ws = pick("v2q", 128, 144, "b2q", (0, 512), T.l2[:, 8:9], c_l)
+    fan_codes("v2q", "lwq", "win", wv, who=(2,))
+    fan_scales("v2q", "lwq", "win", ws, who=(2,))
+    wo = pick("lwq", 144, 192, "b2q", (0, 512), T.l2b[:, 0:3], c_l2)
     c_ln3 = act(T.ln[:, 96:104], T.nbf[:, 8:16], F.Copy, c_nb, c_ln)
 
+    vo = pick("lvq", 144, 192, "p1q", (0, 128), T.l1b[:, 0:3], c_lb)
     c_q = quant(T.wq[:], T.wqs[:], T.wb[:], ("dw", 16))
-    c_wt = fill(T.wt[:], -1.0)
-    ov, os_ = pick("o1q", 0, 192, "lvq", 208, T.pl[:, 0:12], c_pl, ("vin", 2 * landing), ("dv", 32), ("dz", 64))
+    ov, os_ = pick("o1q", 0, 192, "lvq", (0, 208), T.pl[:, 0:12], c_pl, ("vin", 2 * landing), vo[0], vo[1], ("dz", 64))
     need("y", ov, os_)
     dma("y", T.oc[:, 0:768], T.o1q[:].bitcast(dt.uint8), "st")
     for k in range(4):
@@ -451,8 +456,8 @@ def rank_program(g, core, T, topo):
     for k, (a, q, i, n, o) in enumerate(((0, 1, 0, 32, 0), (0, 2, 0, 16, 32), (1, 1, 16, 16, 0), (1, 2, 0, 32, 16),
                                          (2, 0, 0, 32, 0), (2, 1, 0, 16, 32), (3, 2, 16, 16, 0), (3, 3, 0, 32, 16))):
         out, in_ = T.wt[0:32, 48 * a + o:48 * a + o + n], T.tr[32 * q:32 * q + 32, 32 * a + i:32 * a + i + n]
-        c_t.append(act(out, in_, F.Copy, c, c_wt) if k % 2 else copy(out, in_, c, c_wt))
-    ov, os_ = pick("o2q", 0, 192, "lwq", 208, T.pl[:, 0:12], ("win", 2 * landing), wo[0], wo[1])
+        c_t.append(act(out, in_, F.Copy, c, c_wt) if k % 3 == 1 else copy(out, in_, c, c_wt))
+    ov, os_ = pick("o2q", 0, 192, "lwq", (0, 208), T.pl[:, 0:12], ("win", 2 * lands((0, 1), (2,))), wo[0], wo[1])
     m = mm(T.psc[:, 0:192], "wq", 0, 128, "o2q", 0, 192, False, True, ov, os_)
     need("y", ov)
     dma("y", T.oc[:, 768:1536], T.o2q[:].bitcast(dt.uint8), "st")

@@ -4,9 +4,24 @@ from concourse.mybir import dt, AluOpType, AxisListType, ActivationFunctionType
 A = AluOpType
 F = ActivationFunctionType
 NR = 4
-OT = 896
+OT = 944
 LOW = -1e29
 RND = 1.5 * 2.0 ** 27
+LAND = 80
+OPT = {}
+ORDER = {
+    "v": "zz gi zo ui tk vl cxc on df cxd ti e0 cxa e4 hi tk2 xq hcol off rsl off1 ua ih ofo rma trq eq eq1 mk hot1 hot epq2 otq epq1 p1q "
+         "epq3 rr b1q3 hc tk1 wl1 nl bb1 bb aa aa1 aa3 aa2 epq abq b1q2 wl2 b1q zl wl wl3 zsc ph1 zo1 ph bm22 zo2 pg1 wlq xpq zoc b1q1 "
+         "zq pl rm rm2 rm3 rm1 b2q1 rm4 rm5 hixaq loxaq b2q2 xaq hixcq b2q loxcq b2q3 l1 xcq rg rg1 ra l11 ra1 rg2 raq rg3 ra2 ra3 vbc "
+         "rcq rm8 rm9 rm6 rm7 vac rm10 rm11 hixaq1 nbz loxaq1 nb3 xaq1 hixcq1 nb5 loxcq1 wq xcq1 l2 voc wac l21 ln2 wbc tr wc9 wc6 wc5 "
+         "wc3 wc4 wc8 woc o1c o2c yl1 ysb1",
+    "s": "co cxb trb epb wlb nf bm13 bm12 bm1 db1 db3 db zss pg bm11 zos bm21 db2 sg sg2 sg3 sg1 sg5 sg4 dq dq2 dq1 gs gs1 dq3 nb1 gs2 "
+         "gs3 nb2 vas vbs vos nb sg8 sg9 sg6 sg7 sg10 sg11 nb4 o1s was ln1 wos wbs wc2 wc7 os wno yl o2s ysb os7 os4",
+    "t": "mc mc1 mu mt mb2 mb1 mb3 ml mb mxpq mxpq1 ma ma2 ma1 mh mh1 mp3 mp2 mp mp1 mxaq mxaq1 mxcq mxcq1 ma5 ma3 ma4 mh2 mh3 mxaq2 "
+         "mxaq3 mxcq2 mxcq3 my mz my1 mz1",
+    "g": "pi im iba rst cel t1 ibb tri eye ofs m16 ln zc zs bm2 bm23 rz wt yz vs vc n wc ws wc1 ws1",
+    "y": "x b1 b2 dz3 dz dz2 dz1 ofa w wn oc os1 os2 os3 oc1 os5 os6 y",
+}
 
 
 def _sb(n, d):
@@ -14,26 +29,27 @@ def _sb(n, d):
 
 
 SCRATCH = {}
-for _n, _w in (("xq", 224), ("wq", 128), ("p1q", 128), ("b1q", 512), ("b2q", 512), ("trq", 256), ("wlq", 128), ("epq", 512),
-               ("otq", 134), ("abq", 140), ("xaq", 136), ("xcq", 132), ("xpq", 140), ("zsq", 144), ("zq", 192), ("vbq", 144), ("lvq", 208),
-               ("v2q", 144), ("lwq", 208), ("raq", 128), ("rcq", 192), ("o1q", 192), ("o2q", 192)):
+for _n, _w in (("xq", 236), ("wq", 128), ("b1q", 512), ("b2q", 512), ("trq", 128), ("wlq", 128), ("epq", 512), ("p1q", 128),
+               ("otq", 128), ("abq", 140), ("xaq", 136), ("xcq", 132), ("xpq", 140), ("zsq", 144), ("zq", 448), ("vbq", 192),
+               ("lvq", 272), ("v2q", 160), ("lwq", 272), ("raq", 128), ("o1q", 192), ("o2q", 192)):
     SCRATCH[_n] = _sb(_w, "float8_e4m3fn_x4")
     SCRATCH[_n + "s"] = _sb(_w, "uint8")
-for _n, _w in (("cx", 976), ("wb", 512), ("pp", 608), ("bm1", 2048), ("trb", 516), ("wlb", 512),
-               ("epb", 516), ("ab", 656), ("rt", 1280), ("zz", 536), ("on1", 128),
-               ("t1", 128), ("im", 128), ("jk1", 1024), ("jk2", 1024), ("nbf", 16), ("ln", 128), ("tr", 128)):
+for _n, _w in (("cx", 1024), ("wb", 512), ("pp", 640), ("pq", 512), ("bm1", 2048), ("bm2", 2048), ("trb", 512), ("wlb", 512),
+               ("epb", 516), ("ab", 656), ("rt", 1024), ("zz", 536), ("on1", 128), ("m16", 12),
+               ("t1", 128), ("im", 128), ("ih", 128), ("jk1", 768), ("jk2", 768), ("nbf", 16), ("ln", 128), ("tr", 128)):
     SCRATCH[_n] = _sb(_w, "bfloat16")
-for _n, _w in (("rst", 10), ("rma", 10), ("ua", 11), ("rr", 10), ("hc", 2), ("nl", 2), ("tk", 4), ("ib", 12), ("f0", 1), ("f1", 1),
-               ("vl", 1), ("mk", 4), ("hcol", 1), ("df", 1), ("e0", 1), ("e4", 1), ("off", 2), ("rm1", 1024), ("rm2", 1024), ("nf", 80),
-               ("tf", 2), ("q1", 2), ("wt", 208), ("wno", 192), ("ysb", 192), ("db", 512), ("dq", 384), ("g2", 192), ("g3", 192)):
+for _n, _w in (("rst", 10), ("rma", 10), ("ua", 11), ("rr", 10), ("hc", 2), ("tk", 3), ("ib", 24),
+               ("vl", 1), ("mk", 4), ("hcol", 1), ("df", 1), ("e0", 1), ("e4", 1), ("off", 2), ("rm1", 768), ("rm2", 768), ("nf", 128),
+               ("wt", 272), ("wno", 192), ("ysb", 192), ("yl", 272), ("db", 512), ("dq", 512), ("gs", 1024)):
     SCRATCH[_n] = _sb(_w, "float32")
-for _n, _w in (("pi", 1), ("pa", 1), ("pb", 1), ("gi", 1), ("ui", 1), ("ti", 1), ("hi", 1), ("vi", 2), ("ai", 2), ("bi", 2), ("t0", 1), ("t2", 1)):
+for _n, _w in (("pi", 1), ("gi", 1), ("ui", 1), ("ti", 1), ("hi", 1), ("t2", 1)):
     SCRATCH[_n] = _sb(_w, "int32")
-for _n, _w in (("zl", 12), ("zl2", 4), ("pl", 12), ("l1", 12), ("l1b", 4), ("l2", 12), ("l2b", 4), ("ofo", 2), ("ofa", 8), ("o2", 2)):
+for _n, _w in (("zl", 12), ("zl2", 8), ("pl", 12), ("l1", 12), ("l2", 12), ("ofo", 2), ("ofa", 8)):
     SCRATCH[_n] = _sb(_w, "uint16")
-for _n in ("psa", "psb", "psc", "psd", "pd0", "pd1", "pd2", "pd3"):
+BANKS = ("psa", "psb", "psc", "psd", "pd0", "pd1", "pd2", "pd3")
+for _n in BANKS:
     SCRATCH[_n] = ("psum", [128, 512], "float32")
-SEMAPHORES = ["qv", "qs", "qt", "qg", "dx", "dco", "dp1", "db2", "dw", "dz", "do", "st", "zin", "vin", "win", "nin", "oin", "left"]
+SEMAPHORES = ["qv", "qs", "qt", "qg", "dx", "dco", "dp1", "db2", "dw", "do", "dz", "st", "zin", "vin", "win0", "win1", "nin", "oin", "left"]
 
 
 def _mask(topo, src, peers, kind, who):
@@ -51,427 +67,427 @@ def _mask(topo, src, peers, kind, who):
     return out
 
 
-def rank_program(g, core, T, topo):
+def r(name, c0=0, c1=None, step=1, p=(0, 128)):
+    return (name, c0, SCRATCH[name][1][1] if c1 is None else c1, step, p, None)
+
+
+def by(win, off):
+    return win[:5] + (off,)
+
+
+def _meet(a, b):
+    return a[0] == b[0] and a[4][0] < b[4][1] and b[4][0] < a[4][1] and not set(range(*a[1:4])).isdisjoint(range(*b[1:4]))
+
+
+def steps_of(g, core, T, topo):
     rank = T.rank_of(core)
-    if rank is None:
-        return
     S = T.sem
-    eng = {"v": g.vector, "s": g.scalar, "t": g.tensor, "g": g, "y": g.sync}
-    qsem = {"v": "qv", "s": "qs", "t": "qt", "g": "qg"}
-    cnt = {"v": 0, "s": 0, "t": 0, "g": 0}
-    seen = {q: {} for q in eng}
-
-    def need(q, *deps):
-        for sem, val in deps:
-            if seen[q].get(sem, 0) < val:
-                eng[q].wait_ge(S[sem], val)
-                seen[q][sem] = val
-
-    def done(q, ins):
-        ins.then_inc(S[qsem[q]], 1)
-        cnt[q] += 1
-        return (qsem[q], cnt[q])
-
     V, SC, TE = g.vector, g.scalar, g.tensor
-    stores = [0]
+    eng = {"v": V, "s": SC, "t": TE, "g": g, "y": g.sync}
+    steps, names = [], {}
 
-    def dma(q, out, in_, sem):
-        eng[q].dma_start(out, in_).then_inc(S[sem], 16)
-        if sem == "st":
-            stores[0] += 1
+    def ap(x, cast=None):
+        if not isinstance(x, tuple):
+            return x
+        v = T[x[0]][x[4][0]:x[4][1], x[1]:x[2]:x[3]] if x[3] > 1 else T[x[0]][x[4][0]:x[4][1], x[1]:x[2]]
+        if cast is not None:
+            v = v.bitcast(cast)
+        return v if x[5] is None else v.indirect(ap(x[5]))
 
-    def ts(out, in0, s1, s2, op0, op1, *deps):
-        need("v", *deps)
-        if op1 is None:
-            return done("v", V.tensor_scalar(out, in0, s1, s2, op0))
-        return done("v", V.tensor_scalar(out, in0, s1, s2, op0, op1))
+    def step(name, qs, make, reads, writes, wait=(), sem=None):
+        names[name] = names.get(name, -1) + 1
+        reads = [x for x in reads if isinstance(x, tuple)]
+        reads += [x[5] for x in reads if x[5] is not None]
+        steps.append({"name": name + (str(names[name]) if names[name] else ""), "qs": qs, "make": make, "r": reads,
+                      "w": [x for x in writes if isinstance(x, tuple)], "wait": list(wait), "sem": sem})
+        return steps[-1]["name"]
 
-    def tt(out, a, b, op, *deps):
-        need("v", *deps)
-        return done("v", V.tensor_tensor(out, a, b, op))
+    def dma(name, qs, out, in_, sem, cast=None, **k):
+        return step(name, qs, lambda q: eng[q].dma_start(ap(out, cast), ap(in_, cast)), [in_], [out], sem=sem, **k)
 
-    def fill(ap, c, *deps):
-        need("v", *deps)
-        return done("v", V.memset(ap, c))
+    def ts(name, out, in0, s1, s2, op0, op1=None, **k):
+        ops = (op0,) if op1 is None else (op0, op1)
+        return step(name, "v", lambda q: V.tensor_scalar(ap(out), ap(in0), ap(s1), ap(s2), *ops), [in0, s1, s2], [out], **k)
 
-    def copy(out, in_, *deps):
-        need("v", *deps)
-        return done("v", V.tensor_copy(out, in_))
+    def tt(name, out, a, b, op, **k):
+        return step(name, "v", lambda q: V.tensor_tensor(ap(out), ap(a), ap(b), op), [a, b], [out], **k)
 
-    def quant(q, s, in_, *deps):
-        need("v", *deps)
-        return done("v", V.quantize_mx(q, s, in_))
+    def times(name, out, in_, c, edge=None):
+        def make(q):
+            if q == "g":
+                return g.affine_select(ap(out), ap(in_), [[0, 512]], A.is_ge, 0.0, *edge)
+            if q == "s":
+                return SC.activation(ap(out), ap(in_), F.Copy, scale=ap(c))
+            return V.tensor_scalar(ap(out), ap(in_), ap(c), None, A.mult)
+        return step(name, "svg" if edge else "sv", make, [in_, c], [out])
 
-    def act(out, in_, func, *deps):
-        need("s", *deps)
-        return done("s", SC.activation(out, in_, func))
+    def fill(name, out, c, qs="vs"):
+        z = r("zz", 0, len(range(*out[1:4])), p=out[4])
 
-    def iota(out, pattern, base):
-        return done("g", g.iota(out, pattern, base, 0, allow_small_or_imprecise_dtypes=True))
+        def make(q):
+            if q == "g":
+                return g.iota(ap(out), [[0, z[2]]], int(c), 0, allow_small_or_imprecise_dtypes=True)
+            return V.memset(ap(out), c) if q == "v" else SC.activation(ap(out), ap(z), F.Identity, bias=c)
+        return step(name, qs + "g" if len(qs) > 1 and c == int(c) and out[4] == (0, 128) else qs, make, [z] if "s" in qs else [], [out])
 
-    def mm(out, name, c0, c1, mov, m0, m1, start, stop, *deps):
-        need("t", *deps)
-        return done("t", TE.matmul_mx(out, T[name][:, c0:c1], T[name + "s"][:, c0:c1], T[mov][:, m0:m1], T[mov + "s"][:, m0:m1], start, stop))
+    def copy(name, out, in_, qs="vs", **k):
+        return step(name, qs, lambda q: V.tensor_copy(ap(out), ap(in_)) if q == "v" else SC.activation(ap(out), ap(in_), F.Copy),
+                    [in_], [out], **k)
 
-    def pick_codes(dst, d0, d1, win, w, lst, *deps):
-        need("v", *deps)
-        return done("v", V.tensor_copy(T[dst][:, d0:d1].bitcast(dt.uint32), T[win][:, w[0]:w[1]].bitcast(dt.uint32).indirect(lst)))
+    def sc(x):
+        return (x[0] + "s",) + x[1:]
 
-    def pick_scales(dst, d0, d1, win, w, lst, *deps):
-        return act(T[dst + "s"][:, d0:d1], T[win + "s"][:, w[0]:w[1]].indirect(lst), F.Copy, *deps)
+    def quant(name, out, in_, **k):
+        return step(name, "v", lambda q: V.quantize_mx(ap(out), ap(sc(out)), ap(in_)), [in_], [out, sc(out)], **k)
 
-    def pick(*a):
-        return pick_codes(*a), pick_scales(*a)
+    def iota(name, out, pattern, base):
+        return step(name, "g", lambda q: g.iota(ap(out), pattern, base, 0, allow_small_or_imprecise_dtypes=True), [], [out])
+
+    def select(name, out, in_, pattern, op, c):
+        return step(name, "g", lambda q: g.affine_select(ap(out), ap(in_), pattern, op, c, 0, -1), [in_], [out])
+
+    def scan(name, out, d0, d1, first=LOW):
+        return step(name, "v", lambda q: V.tensor_tensor_scan(ap(out), ap(d0), ap(d1), first, A.add, A.max), [d0, d1], [out])
+
+    def mm(name, bank, a, b, start, stop, **k):
+        out = r(bank, 0, b[2] - b[1])
+        return step(name, "t", lambda q: TE.matmul_mx(ap(out), ap(a), ap(sc(a)), ap(b), ap(sc(b)), start, stop),
+                    [a, sc(a), b, sc(b)], [out], **k)
+
+    def pick(name, out, win, lst, **k):
+        step(name + "c", "v", lambda q: V.tensor_copy(ap(out, dt.uint32), ap(by(win, lst), dt.uint32)), [by(win, lst)], [out], **k)
+        copy(name + "s", sc(out), by(sc(win), lst), qs="sv", **k)
 
     ALL = (0, 1, 2)
     peers = [T.cores[(rank + 1 + a) % NR] for a in ALL]
 
-    def lands(*whos):
-        n = 0
-        for c in peers:
-            for who in whos:
-                n += len(_mask(topo, c, [T.cores[(T.rank_of(c) + 1 + a) % NR] for a in ALL], 0, who).get(core, ()))
-        return n
+    def lands(who):
+        return sum(len(_mask(topo, c, [T.cores[(T.rank_of(c) + 1 + a) % NR] for a in ALL], 0, who).get(core, ())) for c in peers)
     landing = lands(ALL)
     left = [0]
 
-    def fan(srcs, dsts, sem, *deps, kind=0, who=ALL):
-        need("g", *deps)
+    def fan(name, srcs, dsts, sem, cast=None, kind=0, who=ALL, **k):
         emask = _mask(topo, core, peers, kind, who)
         tr = []
         for a in who:
             c = peers[a]
             rid, pid, _ = topo.addr(c)
             tr.append(RemoteDMATransfer(dst_ids=[DstId(rid=rid, pnc=pid)], dma_engine_mask=sum(1 << e for e in emask[c]),
-                                        remote_sem=S[sem], srcs=[srcs[a]], dsts=[dsts[a]]))
+                                        remote_sem=S[sem], srcs=[ap(srcs[a], cast)], dsts=[ap(dsts[a], cast)]))
             left[0] += len(emask[c])
-        g.remote_dma_fused(tr, local_sem=S["left"])
+        return step(name, "g", lambda q: g.remote_dma_fused(tr, local_sem=S["left"]), [srcs[a] for a in who], [], sem="left", **k)
 
-    def fan_codes(src, dst, sem, *c, who=ALL):
-        fan([T[src][:, 48 * a:48 * a + 48].bitcast(dt.uint8) for a in ALL],
-            [T[dst][:, 48 * (2 - a):48 * (2 - a) + 48].bitcast(dt.uint8) for a in ALL], sem, *c, who=who)
+    def send(name, src, at, dst, to, sem, who=ALL, **k):
+        s, d = [r(src, at[a], at[a] + 48) for a in ALL], [r(dst, to[2 - a], to[2 - a] + 48) for a in ALL]
+        fan(name + "c", s, d, sem, cast=dt.uint8, who=who, **k)
+        fan(name + "s", [sc(x) for x in s], [sc(x) for x in d], sem, kind=1, who=who, **k)
+    BACK = (LAND, LAND + 48, LAND + 96)
 
-    def fan_scales(src, dst, sem, *c, who=ALL):
-        fan([T[src + "s"][:, 48 * a:48 * a + 48] for a in ALL], [T[dst + "s"][:, 48 * (2 - a):48 * (2 - a) + 48] for a in ALL], sem, *c,
-            kind=1, who=who)
+    dma("x", "y", r("cx", 128, 896), T.x[:], "dx")
+    dma("co", "s", r("cx", 24, 40), T.co[:, 0:4 * NR], "dco")
+    dma("b1", "y", r("pp", 96, 608), T.b1[:], "dp1")
+    dma("b2", "y", r("pq"), T.b2[:], "db2")
 
-    dma("y", T.cx[:, 128:OT], T.x[:], "dx")
-    dma("s", T.cx[:, 24:40], T.co[:, 0:4 * NR], "dco")
-    dma("y", T.pp[:, 64:576], T.b1[:], "dp1")
-
-    c_pi = done("g", g.iota(T.pi[:], [[0, 1]], 0, 1))
-    c_on = fill(T.on1[:], 1.0)
-    c_zz = fill(T.zz[:], 0.0)
-    need("s", c_zz)
-    c_tr = done("s", SC.activation(T.trb[:], T.zz[:, 0:516], F.Identity, bias=1.0))
-    c_ua = act(T.ua[:], T.zz[:, 0:11], F.Copy)
-    c_e0 = act(T.epb[:], T.zz[:, 0:516], F.Copy)
-    c_w0 = act(T.wlb[:], T.zz[:, 0:512], F.Copy)
-    c_ln = act(T.ln[:], T.zz[:, 0:128], F.Copy)
-    need("g", c_on)
-    c_t1 = done("g", g.affine_select(T.t1[:], T.on1[:], [[1, 128]], A.is_gt, 0.0, 0, -1))
+    step("pi", "g", lambda q: g.iota(T.pi[:], [[0, 1]], 0, 1), [], [r("pi")])
+    fill("zz", r("zz"), 0.0, "v")
+    fill("on", r("on1"), 1.0)
+    fill("trb", r("trb"), 1.0, "sv")
+    fill("ua", r("ua"), 0.0, "sv")
+    fill("nf", r("nf"), 0.0, "sv")
+    fill("epb", r("epb"), 0.0, "sv")
+    select("t1", r("t1"), r("on1"), [[1, 128]], A.is_gt, 0.0)
+    iota("im", r("im"), [[0, 8], [1, 16]], 0)
+    step("ih", "sv", lambda q: SC.activation(T.ih[:], T.im[:], F.Identity, bias=-7.5) if q == "s" else
+         V.tensor_scalar(T.ih[:], T.im[:], -7.5, None, A.add), [r("im")], [r("ih")])
+    fill("wlb", r("wlb"), 0.0, "sv")
+    c_ln = fill("ln", r("ln"), 0.0, "sv")
     if rank < NR - 1:
-        iota(T.ib[:, 0:9 - 3 * rank], [[256, 3 - rank], [16, 3]], 1280 + 256 * rank)
-    c_ib = iota(T.ib[:, 9 - 3 * rank:12], [[256, rank + 1], [16, 3]], 1024)
-    c_im = iota(T.im[:], [[0, 8], [1, 16]], 0)
-    ts(T.gi[:], T.pi[:], 4, None, A.arith_shift_right, None, c_pi)
-    c = ts(T.ui[:], T.pi[:], 2, 3, A.arith_shift_right, A.bitwise_and)
-    ts(T.ti[:], T.pi[:], 3 if rank < 2 else 0, None, A.bitwise_and, None)
-    c_hi = ts(T.hi[:], T.pi[:], 5, None, A.arith_shift_right, None)
-    c = tt(T.df[:], T.gi[:], T.ui[:], A.subtract, c)
-    fill(T.cx[:, 0:24], 0.0)
-    c_hcol = ts(T.hcol[:], T.hi[:], 128.0, None, A.mult, None, c_hi)
-    if rank % 2 == 0:
-        ts(T.e0[:], T.df[:], 0.0, None, A.is_equal, None, c)
-    c = ts(T.e4[:], T.df[:], 4.0, None, A.is_equal, None, c)
-    c_cb = fill(T.cx[:, 40:128], 0.0)
-    c_ot = fill(T.cx[:, OT:OT + 80], 0.0)
-    c_tr = fill(T.trb[:, 2:516:4], 0.0, c_tr)
-    for k, (e, v) in enumerate((((T.e0, -8.0), (T.e4, -8.0)), ((T.e4, -4.0),))[rank % 2]):
-        c = ts(T.off[:, k:k + 1], T.ti[:], v, e[:], A.add, A.mult, c)
+        iota("iba", r("ib", 0, 18 - 6 * rank), [[256, 3 - rank], [16, 3], [0, 2]], 1280 + 256 * rank)
+    iota("ibb", r("ib", 18 - 6 * rank, 24), [[256, rank + 1], [16, 3], [0, 2]], 1024)
+    ts("gi", r("gi"), r("pi"), 4, None, A.arith_shift_right)
+    ts("ui", r("ui"), r("pi"), 2, 3, A.arith_shift_right, A.bitwise_and)
+    ts("ti", r("ti"), r("pi"), (3, 1, 0, 0)[rank], None, A.bitwise_and)
+    ts("hi", r("hi"), r("pi"), 5, None, A.arith_shift_right)
+    tt("df", r("df"), r("gi"), r("ui"), A.subtract)
+    fill("cxa", r("cx", 0, 24), 0.0)
+    ts("hcol", r("hcol"), r("hi"), 128.0, None, A.mult)
+    if rank == 1:
+        ts("e0", r("t2"), r("pi"), 1, 1, A.arith_shift_right, A.bitwise_and)
+        ts("e4", r("e4"), r("t2"), 4.0, r("df"), A.mult, A.is_equal)
+    else:
+        if rank < 3:
+            ts("e0", r("e0"), r("df"), 0.0, None, A.is_equal)
+        ts("e4", r("e4"), r("df"), 4.0, None, A.is_equal)
+    fill("cxb", r("cx", 40, 128), 0.0)
+    fill("cxc", r("cx", 896, OT + 80), 0.0)
+    none = (8.0, 8.0, 24.0, 24.0)[rank]
+    for k, e in enumerate((("e0", "e4"), ("e4",))[rank % 2]):
+        ts("off", r("off", k, k + 1), r("ti"), (0.0, 4.0, 11.0, 23.0)[rank] - none, r(e), A.add, A.mult)
     wide = 2 - rank % 2
-    c_rs = fill(T.rst[:], 0.0)
-    c_of = ts(T.ofo[:, 0:wide], T.off[:, 0:wide], 8.0, None, A.add, None, c)
-    c_rs = fill(T.rst[:, 4:7], LOW, c_rs)
-    c_mk = ts(T.mk[:], T.im[:, 0:4], 128.0, T.hcol[:], A.mult, A.is_equal, c_im, c_hcol)
-    need("g", c_t1, c_tr)
-    c_tri = done("g", g.affine_select(T.trb[:, 1:513:4], T.t1[:], [[1, 128]], A.not_equal, 1024.0, 0, -1))
-    need("g", c_ot)
-    c_oi = iota(T.cx[:, OT + 27:OT + 75:4], [[0, 2], [2, 6]], 0)
-    own = slice(2 * rank, 2 * rank + wide)
-    fan([T.ofo[:, 0:wide]] * 3, [T.ofa[:, own]] * 3, "oin", c_of)
-    need("y", c_of)
-    dma("y", T.ofa[:, own], T.ofo[:, 0:wide], "do")
-    need("g", c_e0)
-    c_ep = done("g", g.affine_select(T.epb[:, 4:516:4], T.on1[:], [[1, 128]], A.is_equal, 0.0, 0, -1))
-
-    need("s", c_mk, ("dp1", 16))
+    fill("rst", r("rst"), 0.0)
+    ts("ofo", r("ofo", 0, wide), r("off", 0, wide), none, None, A.add)
+    fill("rsl", r("rst", 4, 7), LOW, "v")
+    ts("mk", r("mk"), r("im", 0, 4), 128.0, r("hcol"), A.mult, A.is_equal)
+    ts("vl", r("vl"), r("pi"), 64.0, None, A.is_ge)
+    fill("cxd", r("cx", 898, OT, 4), -7.5 / 128)
+    quant("zq", r("zq", 256, 384), r("zz", 0, 512))
+    select("tri", r("trb", 0, 512, 4), r("t1"), [[1, 128]], A.not_equal, 1024.0)
+    iota("cel", r("cx", 899, OT, 4), [[0, 2], [2, 6]], 0)
+    fan("ofs", [r("ofo", 0, wide)] * 3, [r("ofa", 2 * rank, 2 * rank + wide)] * 3, "oin")
+    OIN = [("oin", landing), dma("ofa", "y", r("ofa", 2 * rank, 2 * rank + wide), r("ofo", 0, wide), "do")]
+    select("eye", r("epb", 4, 516, 4), r("on1"), [[1, 128]], A.is_equal, 0.0)
+    EDGE = {0: (31, -1), 3: (-96, 1)}
     for h in range(4):
-        c_m1 = done("s", SC.activation(T.bm1[:, 512 * h:512 * h + 512], T.pp[:, 64:576], F.Copy, scale=T.mk[:, h:h + 1]))
+        times("bm1", r("bm1", 512 * h, 512 * h + 512), r("pp", 96, 608), r("mk", h, h + 1), EDGE.get(h))
+    for h in range(4):
+        times("bm2", r("bm2", 512 * h, 512 * h + 512), r("pq"), r("mk", h, h + 1), EDGE.get(h))
 
-    c_x = quant(T.xq[:], T.xqs[:], T.cx[:, 0:OT], ("dco", 16), c_cb, ("dx", 16))
-    need("y", c_x)
+    quant("xq", r("xq"), r("cx", 0, OT))
     for b in ("lvq", "lwq"):
-        dma("y", T[b][:, 192:208].bitcast(dt.uint8), T.xq[:, 16:32].bitcast(dt.uint8), "dz")
-        dma("y", T[b + "s"][:, 192:208], T.xqs[:, 16:32], "dz")
-    mm(T.psa[:, 0:128], "xq", 32, 160, "xq", 6, 134, True, False, c_x)
-    m = mm(T.psa[:, 0:128], "xq", 96, 224, "xq", 0, 128, False, True)
-    c_vl = ts(T.vl[:], T.pi[:], 64.0, None, A.is_ge, None)
-    c_o1 = fill(T.cx[:, OT + 1:OT + 64:4], -7.5 / 128, c_ot)
-    for k in range(2):
-        quant(T.trq[:, 128 * k:128 * k + 128], T.trqs[:, 128 * k:128 * k + 128], T.trb[:, 1 + 2 * k:513 + 2 * k], c_tri)
-
-    def scan(out, d0, d1, *deps):
-        need("v", *deps)
-        return done("v", V.tensor_tensor_scan(out, d0, d1, LOW, A.add, A.max))
-    s = scan(T.rma[:], T.rst[:], T.psa[:, 0:10], m, c_rs)
-    ts(T.pa[:], T.pi[:], 112, None, A.bitwise_and, None)
-    u = ts(T.ua[:, 1:5], T.rma[:, 0:4], T.rma[:, 3:4], None, A.is_equal, None, s, c_ua)
-    u = ts(T.ua[:, 7:11], T.rma[:, 6:10], T.rma[:, 9:10], T.vl[:], A.is_equal, A.mult, c_vl)
-    c_pb = ts(T.pb[:], T.pi[:], 15, None, A.bitwise_and, None)
-    o = tt(T.cx[:, OT + 24:OT + 64:4], T.ua[:, 1:11], T.ua[:, 0:10], A.subtract, u, c_o1)
-    c_o = quant(T.otq[:], T.otqs[:], T.cx[:, OT + 64 - 536:OT + 64], o, c_oi)
-    mm(T.psc[:, 0:128], "trq", 0, 128, "otq", 6, 134, True, False, c_o)
-    m = mm(T.psc[:, 0:128], "trq", 128, 256, "otq", 0, 128, False, True)
-    ts(T.tk[:, 2:3], T.pa[:], 64.0, T.vl[:], A.add, A.mult, c_pb)
-    ts(T.tk[:, 3:4], T.pb[:], T.vl[:], None, A.mult, None)
-    copy(T.tk[:, 0:1], T.pa[:])
-    c_tk = copy(T.tk[:, 1:2], T.pb[:])
-    ts(T.t0[:], T.pi[:], 1, None, A.bitwise_and, None)
-    ct = ts(T.t2[:], T.pi[:], 1, 1, A.arith_shift_right, A.bitwise_and)
-    r = scan(T.rr[:], T.rst[:], T.psc[:, 118:128], m)
-    c_hc = ts(T.hc[:], T.rr[:, 3:10:6], RND, RND, A.add, A.subtract, r)
-    c_nl = tt(T.nl[:], T.hc[:], T.rr[:, 3:10:6], A.subtract, c_hc)
+        dma("dz", "y", r(b, 0, 16), r("xq", 16, 32), "dz", cast=dt.uint8)
+        dma("dz", "y", r(b + "s", 0, 16), r("xqs", 16, 32), "dz")
+    mm("mc", "psa", r("xq", 32, 160), r("xq", 6, 134), True, False)
+    mm("mc", "psa", r("xq", 96, 224), r("xq", 0, 128), False, True)
+    quant("trq", r("trq"), r("trb"))
+    scan("rma", r("rma"), r("rst"), r("psa", 0, 10))
+    ts("eq", r("ua", 1, 5), r("rma", 0, 4), r("rma", 3, 4), None, A.is_equal)
+    ts("eq", r("ua", 7, 11), r("rma", 6, 10), r("rma", 9, 10), r("vl"), A.is_equal, A.mult)
+    tt("hot", r("cx", OT + 24, OT + 64, 4), r("ua", 1, 11), r("ua", 0, 10), A.subtract)
+    tt("hot", r("cx", OT + 49, OT + 64, 4), r("ua", 1, 5), r("ua", 0, 4), A.subtract)
+    quant("otq", r("otq"), r("cx", OT + 64 - 512, OT + 64))
+    mm("mu", "psc", r("trq"), r("xq", 106, 234), True, False)
+    mm("mt", "psc", r("trq"), r("otq"), False, True)
+    ts("tk", r("tk", 0, 1), r("gi"), 16.0, None, A.mult)
+    ts("tk", r("tk", 1, 2), r("gi"), 16.0, 64.0, A.mult, A.add)
+    tt("tk", r("tk", 2, 3), r("pi"), r("tk", 0, 1), A.subtract)
+    fill("m16", r("m16"), -16.0)
+    scan("rr", r("rr"), r("rst"), r("psc", 118, 128))
+    ts("hc", r("hc"), r("rr", 3, 10, 6), RND, RND, A.add, A.subtract)
+    tt("nl", r("nf", 107, 120, 12), r("rr", 3, 10, 6), r("hc"), A.subtract)
+    for s in range(2):
+        ts("bb", r("ab", 512 + s, 560, 2), r("ib"), r("hc", s, s + 1), 256.0, A.is_equal, A.mult)
     for t in range(4):
-        ts(T.ab[:, 512 + t:560:4], T.ib[:], T.hc[:, t // 2:t // 2 + 1], T.tk[:, t:t + 1], A.is_equal, A.mult, c_tk, c_ib)
-    for t in range(4):
-        c_a = ts(T.ab[:, t:512:4], T.im[:], T.nl[:, t // 2:t // 2 + 1], 7.5, A.add, A.is_equal, c_nl, c_im)
-    c_a = quant(T.abq[:], T.abqs[:], T.ab[:, 0:560], c_a)
-    m0 = mm(T.psa[:, 0:128], "abq", 0, 128, "abq", 12, 140, True, True, c_a)
-
-    def e_tile(b):
-        return quant(T.epq[:, 128 * b:128 * b + 128], T.epqs[:, 128 * b:128 * b + 128], T.epb[:, 4 - b:516 - b], c_ep)
-    c_e = [e_tile(0), e_tile(1)]
-    c_l = copy(T.zl[:, 0:9], T.psa[:, 116:125], m0)
-    zv, zs = pick("zsq", 0, 144, "xq", (32, 224), T.zl[:, 0:9], c_l)
-    fan_codes("zsq", "zq", "zin", zv, c_ln)
-    fan_scales("zsq", "zq", "zin", zs)
-    iota(T.rt[:, 512:768], [[0, 256]], 0)
-    c_rz = iota(T.rt[:, 1024:1280], [[0, 256]], 0)
-    c_l = copy(T.zl2[:, 0:3], T.psa[:, 125:128])
-    c_p1 = quant(T.p1q[:], T.p1qs[:], T.pp[:, 64:576], ("dp1", 16))
-    zo = pick("zq", 144, 192, "xq", (32, 224), T.zl2[:, 0:3], c_l)
-
-    c_b1 = quant(T.b1q[:], T.b1qs[:], T.bm1[:], c_m1)
-    need("y", c_b1)
+        k = 107 + 12 * (t % 2)
+        ts("aa", r("ab", t, 512, 4), r("ih"), r("nf", k, k + 1), r("tk", min(t, 2), min(t, 2) + 1), A.is_equal, A.mult)
+    quant("abq", r("abq"), r("ab", 0, 560))
+    mm("ml", "psa", r("abq", 0, 128), r("abq", 12, 140), True, True)
+    ts("zl", r("zl", 0, 9), r("psa", 116, 125), 1.0 / 256, None, A.mult)
+    pick("zs", r("zsq"), r("xq", 32, 224), r("zl", 0, 9))
+    send("z", "zsq", (0, 48, 96), "zq", (0, 48, 208), "zin", wait=[c_ln])
+    ZIN = [("zin", 2 * landing)]
+    fill("rz", r("rt", 768, 1024), 0.0)
+    fill("zo", r("zl2", 2, 6), 16, "v")
+    ts("zo", r("zl2", 0, 2), r("psa", 125, 127), 1.0 / 256, 32.0, A.mult, A.add)
+    ts("zo", r("zl2", 6, 7), r("psa", 127, 128), 1.0 / 256, 32.0, A.mult, A.add)
+    pick("zo", r("zq", 96, 208), r("xq", 0, 224), r("zl2", 0, 7))
     for h in range(4):
-        dma("y", T.bm1[32 * h:32 * h + 32, 512 * h:512 * h + 512], T.b2[32 * h:32 * h + 32, :], "db2")
-    need("y", ("zin", 2 * landing))
-    dma("y", T.wb[:], T.w[:], "dw")
-    c_db = []
-
-    def table(b):
-        m = mm(T["pd%d" % b][:, 0:128], "epq", 128 * b, 128 * b + 128, "p1q", 0, 128, True, True, c_e[b], c_p1)
-        need("s", m)
-        c_db.append(done("s", SC.activation(T.db[:, 128 * b:128 * b + 128], T["pd%d" % b][:, 0:128], F.Copy, scale=-1.0)))
-    c_f = act(T.nf[:], T.zz[:, 0:80], F.Copy)
-    table(0)
-    table(1)
-    c_e.append(e_tile(2))
-    c_e.append(e_tile(3))
-    table(2)
-    table(3)
-    c_wt = done("s", SC.activation(T.wt[:], T.zz[:, 0:208], F.Identity, bias=-1.0))
-
-    def book2(h, *deps):
-        return quant(T.b2q[:, 128 * h:128 * h + 128], T.b2qs[:, 128 * h:128 * h + 128], T.bm1[:, 512 * h:512 * h + 512], *deps)
-    c = ts(T.vi[:], T.rr[:, 3:10:6], -1016.5 + 256 * (3 - rank), None, A.add, None)
-    ct = ts(T.f0[:], T.t0[:], 4.0, T.df[:], A.mult, A.is_equal, ct)
+        quant("b1q", r("b1q", 128 * h, 128 * h + 128), r("bm1", 512 * h, 512 * h + 512))
+    dma("w", "y", r("wb"), T.w[:], "dw", wait=ZIN)
     for t in range(4):
-        c_w = ts(T.wlb[:, 129 * t:128 * t + 128:4], T.im[:, 0:32], T.tk[:, 1:2], None, A.is_equal, None, c_w0)
-    ct = ts(T.f1[:], T.t2[:], -4.0, T.f0[:], A.add, A.mult, ct)
-    ts(T.ai[:], T.vi[:], 8, 3, A.arith_shift_right, A.bitwise_and, c)
-    c_bi = ts(T.bi[:], T.vi[:], 255, None, A.bitwise_and, None)
-    c_w = quant(T.wlq[:], T.wlqs[:], T.wlb[:], c_w)
+        ts("wl", r("wlb", 129 * t, 128 * t + 128, 4), r("im", 0, 32), r("tk", 2, 3), None, A.is_equal)
+    quant("wlq", r("wlq"), r("wlb"))
+    for b in range(4):
+        quant("epq", r("epq", 128 * b, 128 * b + 128), r("epb", 4 - b, 516 - b))
+    quant("p1q", r("p1q"), r("pp", 96, 608))
+    for b in range(4):
+        mm("mb", "pd%d" % b, r("epq", 128 * b, 128 * b + 128), r("p1q"), True, True)
+        times("db", r("db", 128 * b, 128 * b + 128), r("pd%d" % b, 0, 128), -1.0)
+    for h in range(4):
+        quant("b2q", r("b2q", 128 * h, 128 * h + 128), r("bm2", 512 * h, 512 * h + 512))
 
-    where = ((("psa", 0), ("psb", 0), ("psc", 0), ("psc", 128)), (("psd", 0), ("psd", 128), ("psd", 256), ("psd", 384)),
-             (("pd0", 0), ("pd1", 0)))
-    N1A, N1C, N2A, N2C, NP = 0, 16, 32, 48, 64
-    O0, O1, OP, O2 = T.ofa[:, 0:2], T.ofa[:, 2:3], T.ofa[:, 4:7], T.o2[:, 0:1]
+    banks = (("psa", "psb", "psc", "psd"), ("pd2", "pd3", "psa", "pd0"))
+    NH, NL = 64, 96
+    O0, O1, OP = r("ofa", 0, 2), r("ofa", 2, 3), r("ofa", 4, 7)
 
-    def scores(k, tok, c0, bk, *deps):
-        if k == 2:
-            return [mm(T["pd%d" % (h // 2)][:, 0:128], tok, 64 - 64 * (h % 2), 192 - 64 * (h % 2), bk, 128 * h, 128 * h + 128,
-                       h % 2 == 0, h % 2 == 1, *deps) for h in range(4)][1::2]
-        if k == 1:
-            return [mm(T.psd[:, 0:512], tok, c0, c0 + 128, bk, 0, 512, True, True, *deps)] * 4
-        m = [mm(T[("psa", "psb")[h]][:, 0:128], tok, c0, c0 + 128, bk, 128 * h, 128 * h + 128, True, True, *deps) for h in range(2)]
-        return m + [mm(T.psc[:, 0:256], tok, c0, c0 + 128, bk, 256, 512, True, True)] * 2
+    def scores0(lv, tok, bk, **k):
+        for h in range(3):
+            mm("ma", banks[lv][h], r(tok, 0, 128), r(bk, 128 * h, 128 * h + 128 + 128 * (h // 2)), True, True, **k)
 
-    def word(k, h, m, rm, jk, at):
-        s = min(k, 1)
-        e = 512 * s + 128 * h
-        b, o = where[k][h]
-        cv = scan(rm[:, e:e + 128], T.zz[:, 0:128], T[b][:, o:o + 128], m[h])
-        need("s", cv, c_f)
-        return cv, done("s", SC.activation(jk[:, e:e + 128], rm[:, e:e + 128], F.Sign, bias=rm[:, e + 127:e + 128], scale=-1.0,
-                                           accum_out=T.nf[:, at + 4 * s + h:at + 4 * s + h + 1]))
+    def scores1(lv, c0, bk, **k):
+        mm("mh", banks[lv][3], r("zq", c0, c0 + 128), r(bk, 0, 256), True, False, **k)
+        mm("mh", banks[lv][3], r("zq", c0 - 64, c0 + 64), r(bk, 256, 512), False, True, **k)
 
-    XT = {"xa": (T.pp, 0, 0, 544), "xc": (T.pp, 576, 80, 608), "xp": (T.ab, 560, 96, 656)}
+    def word(lv, k):
+        e, rm, jk = 128 * k, "rm%d" % (lv + 1), "jk%d" % (lv + 1)
+        b, o = banks[lv][(0, 1, 2, 2, 3, 3)[k]], (0, 0, 0, 128, 0, 128)[k]
+        at = 32 * lv + 16 * (k // 4) + k
+        run, top, fl, n = r(rm, e, e + 128), r(rm, e + 127, e + 128), r(jk, e, e + 128), r("nf", at, at + 1)
+        scan("rm", run, r("zz", 0, 128), r(b, o, o + 128))
+        step("sg", "s", lambda q: SC.activation(ap(fl), ap(run), F.Sign, bias=ap(top), scale=-1.0, accum_out=ap(n)), [run], [fl, n])
 
-    def part_hi(at, off, xt, n, *deps):
-        need("v", *deps)
-        buf, o = XT[xt][0:2]
-        return done("v", V.tensor_scalar(buf[:, o:o + n], T.nf[:, at:at + 16].indirect(off), RND, RND, A.add, A.subtract))
+    def tolist(at, off, buf, o, w0, xt, bank):
+        n = 16 * (off[2] - off[1])
+        win = by(r("nf", at, at + 16), off)
+        ts("hi" + xt, r(buf, o, o + n), win, RND, RND, A.add, A.subtract, wait=OIN)
+        tt("lo" + xt, r(buf, o + n, o + 2 * n), win, r(buf, o, o + n), A.subtract, wait=OIN)
+        added(buf, w0, xt, n // 4, bank)
 
-    def part_lo(at, off, xt, n, c):
-        need("v", c)
-        buf, o = XT[xt][0:2]
-        return done("v", V.tensor_tensor(buf[:, o + n:o + 2 * n], T.nf[:, at:at + 16].indirect(off), buf[:, o:o + n], A.subtract))
+    def added(buf, w0, xt, w, bank):
+        quant(xt, r(xt, 0, 128 + w), r(buf, w0, w0 + 512 + 4 * w))
+        mm("m" + xt, bank, r("wlq"), r(xt, 0, 128), True, False)
+        mm("m" + xt, bank, r("wlq"), r(xt, w, 128 + w), False, True)
 
-    def part_q(xt, c):
-        buf, _, w0, w1 = XT[xt]
-        return quant(T[xt + "q"][:], T[xt + "qs"][:], buf[:, w0:w1], c)
+    def listed(lv, dst, src):
+        if lv == 0:
+            copy("l1", dst, src, "v")
+        else:
+            ts("l2", dst, src, r("hcol"), None, A.add)
 
-    def tolist(bank, xt, w, *deps):
-        mm(bank[:, 0:128], "wlq", 0, 128, xt + "q", 0, 128, True, False, *deps)
-        return mm(bank[:, 0:128], "wlq", 0, 128, xt + "q", w, 128 + w, False, True)
+    def lists(lv, ba, bc):
+        l = "l%d" % (lv + 1)
+        tolist(32 * lv, O0, "pp", 32, 32, "xaq", ba)
+        listed(lv, r(l, 0, 8), r(ba, 0, 8))
+        tolist(32 * lv + 16, O1, "pp", 608, 112, "xcq", bc)
+        listed(lv, r(l, 8, 12), r(bc, 124, 128))
 
-    def unpack(b):
-        return mm(T["pd%d" % b][:, 0:192], "epq", 128 * b, 128 * b + 128, "zq", 0, 192, True, True, c_db[b])
+    def unpacked(b, s):
+        return r("pd%d" % b, 192 * s, 128 + 128 * s)
 
-    ma = scores(0, "zq", 0, "b1q", ("zin", 2 * landing), zo[0], zo[1], c_b1)
-    mc = scores(1, "zq", 64, "b1q")
-    md = [unpack(b) for b in range(4)]
-    word(0, 0, ma, T.rm1, T.jk1, N1A)
-    cq1 = ts(T.q1[:], T.ai[:], 48.0, -192.0, A.mult, A.add, c_bi)
-    word(0, 1, ma, T.rm1, T.jk1, N1A)
-    ts(T.tf[:], T.bi[:], 48.0, None, A.is_lt, None)
-    cq1 = tt(T.q1[:], T.q1[:], T.bi[:], A.add, cq1)
-    word(0, 2, ma, T.rm1, T.jk1, N1A)
-    c_pf = tt(T.nf[:, 64:72:4], T.q1[:], T.tf[:], A.mult, cq1, c_f)
-    _, sa = word(0, 3, ma, T.rm1, T.jk1, N1A)
-    cx = part_hi(NP, OP, "xp", 48, c_pf, ("oin", landing), ("do", 16))
-    word(1, 0, mc, T.rm1, T.jk1, N1C)
-    cx = part_lo(NP, OP, "xp", 48, cx)
-    word(1, 1, mc, T.rm1, T.jk1, N1C)
-    book2(0, ("db2", 64))
-    c = part_hi(N1A, O0, "xa", 32, sa)
-    word(1, 2, mc, T.rm1, T.jk1, N1C)
-    c = part_lo(N1A, O0, "xa", 32, c)
-    _, sc = word(1, 3, mc, T.rm1, T.jk1, N1C)
-    c = part_q("xa", c)
-    la = tolist(T.psa, "xa", 8, c, c_w)
-    cx = part_q("xp", cx)
-    book2(1)
-    book2(2)
-    c_d = [act(T.dq[:, 192 * b:192 * b + 192], T["pd%d" % b][:, 0:192], F.Copy, md[b]) for b in range(2)]
-    c = part_hi(N1C, O1, "xc", 16, sc)
-    c_la = copy(T.l1[:, 0:8], T.psa[:, 0:8], la)
-    c = part_lo(N1C, O1, "xc", 16, c)
-    c_b2 = book2(3)
-    c = part_q("xc", c)
-    lc = tolist(T.psb, "xc", 4, c)
-    mp = tolist(T.psd, "xp", 12, cx)
+    def rest(b, s):
+        out, lst = r("rt", 512 * s + b, 512 + 256 * s, 4), r("l1", 8 * s, 8 + 4 * s)
+        tab, o = by(r("db", 128 * b, 128 * b + 128), lst), 256 * b + 128 * s
+        if b < 2:
+            tt("rg", out, tab, r("dq", o, o + 128 - 64 * s), A.add)
+        else:
+            copy("gs", r("gs", o, o + 128 - 64 * s), tab, "sv")
+            tt("ra", out, r("gs", o, o + 128 - 64 * s), unpacked(b, s), A.add)
 
-    def rest_gather(d0, d1, lst, *c):
-        need("v", *c)
-        for b in range(2):
-            need("v", c_d[b])
-            done("v", V.tensor_tensor(T.rt[:, 6 * d0 + b:2 * d0 + 4 * d1:4], T.db[:, 128 * b:128 * b + 128].indirect(lst),
-                                      T.dq[:, 192 * b + d0:192 * b + d1], A.add))
-        return [act(T["g%d" % b][:, d0:d1], T.db[:, 128 * b:128 * b + 128].indirect(lst), F.Copy, c[0]) for b in (2, 3)]
+    def numbers(lv):
+        c = 32 * lv + 20
+        copy("nb", r("nbf", 4 * lv, 4 * lv + 4), r("nf", 32 * lv, 32 * lv + 4), "sv")
+        copy("nb", r("nbf", 8 + 4 * lv, 10 + 4 * lv, p=(0, 64)), r("nf", c, c + 2, p=(0, 64)), "sv")
+        copy("nb", r("nbf", 10 + 4 * lv, 12 + 4 * lv, p=(0, 64)), r("nf", c, c + 2, p=(64, 128)), "sv")
 
-    def rest_add(d0, d1, cg):
-        for b in (2, 3):
-            c = tt(T.rt[:, 6 * d0 + b:2 * d0 + 4 * d1:4], T["g%d" % b][:, d0:d1], T["pd%d" % b][:, d0:d1], A.add, cg[b - 2], md[b])
-        return c
+    for s in range(2):
+        scan("ph", r("nf", NH + 12 * s, NH + 12 * s + 12), r("m16"), r("ab", 512 + s, 560, 4), first=0.0)
+    copy("pg", r("ab", 608, 656), by(r("nf", NL, NL + 32), OP), wait=OIN)
+    copy("pg", r("ab", 560, 608), by(r("nf", NH, NH + 32), OP), wait=OIN)
+    added("ab", 96, "xpq", 12, "psd")
+    ts("pl", r("pl"), r("psd", 116, 128), 7.5, None, A.add)
 
-    def part_v(k, f):
-        return f("vbq", 64 * k, min(64 * k + 64, 144), "p1q", (0, 128), T.l1[:, 4 * k:min(4 * k + 4, 9)])
-    cg = rest_gather(0, 128, T.l1[:, 0:8], c_la)
-    part_v(0, pick_scales)
-    part_v(1, pick_scales)
-    act(T.nbf[:, 0:4], T.nf[:, 0:4], F.Copy, sc)
-    c_n1 = act(T.nbf[:, 8:16], T.nf[:, 20:28], F.Copy)
-    c_l = copy(T.l1[:, 8:12], T.psb[:, 124:128], lc)
-    c = rest_add(0, 128, cg)
-    c_lb = copy(T.l1b[:, 0:3], T.psb[:, 125:128])
-    c_r = quant(T.raq[:], T.raqs[:], T.rt[:, 0:512], c)
-    ma = scores(0, "raq", 0, "b2q", c_r, c_lb, c_b2)
-    cg = rest_gather(128, 192, T.l1[:, 8:12], c_l, c_rz)
-    vs = part_v(2, pick_scales)
-    fan_scales("vbq", "lvq", "vin", vs)
-    word(0, 0, ma, T.rm2, T.jk2, N2A)
-    c = rest_add(128, 192, cg)
-    word(0, 1, ma, T.rm2, T.jk2, N2A)
-    c_r2 = quant(T.rcq[:], T.rcqs[:], T.rt[:, 512:1280], c)
-    mc = scores(2, "rcq", 0, "b2q", c_r2)
-    word(0, 2, ma, T.rm2, T.jk2, N2A)
-    part_v(0, pick_codes)
-    _, sa = word(0, 3, ma, T.rm2, T.jk2, N2A)
-    part_v(1, pick_codes)
-    word(2, 0, mc, T.rm2, T.jk2, N2C)
-    vv = part_v(2, pick_codes)
-    fan_codes("vbq", "lvq", "vin", vv)
-    vc, sc = word(2, 1, mc, T.rm2, T.jk2, N2C)
-    c = part_hi(N2A, O0, "xa", 32, sa)
-    c_o2 = ts(T.o2[:, 0:1], T.f1[:], 8.0, None, A.add, None, ct)
-    c = part_lo(N2A, O0, "xa", 32, c)
-    c = part_q("xa", c)
-    la = tolist(T.psa, "xa", 8, c)
-    c = part_hi(N2C, O2, "xc", 16, sc, c_o2)
-    c_pl = ts(T.pl[:], T.psd[:, 116:128], 192.0, None, A.add, None, mp)
-    c = part_lo(N2C, O2, "xc", 16, c)
-    c = part_q("xc", c)
-    lc = tolist(T.psb, "xc", 4, c)
-    c_l = ts(T.l2[:, 0:8], T.psa[:, 0:8], T.hcol[:], None, A.add, None, la, c_hcol)
-    act(T.nbf[:, 4:8], T.nf[:, 32:36], F.Copy, sc, c_n1)
-    act(T.nbf[32:64, 12:16], T.nf[96:128, 32:36], F.Copy)
-    act(T.nbf[64:128, 12:16:2], T.nf[0:64, 52:54], F.Copy)
-    c_nb = act(T.nbf[64:128, 13:16:2], T.nf[64:128, 52:54], F.Copy)
-    fan([T.nbf[:, 8 * (a // 2):8 * (a // 2) + 8] for a in ALL], [T.ln[:, 32 * (2 - a):32 * (2 - a) + 8] for a in ALL], "nin", c_nb)
-    wv, ws = pick("v2q", 0, 128, "b2q", (0, 512), T.l2[:, 0:8], c_l)
-    fan_codes("v2q", "lwq", "win", wv, who=(0, 1))
-    fan_scales("v2q", "lwq", "win", ws, who=(0, 1))
-    c_l = ts(T.l2[:, 8:9], T.psb[:, 124:125], T.hcol[:], None, A.add, None, lc)
-    c_l2 = ts(T.l2b[:, 0:3], T.psb[:, 125:128], T.hcol[:], None, A.add, None)
-    wv, ws = pick("v2q", 128, 144, "b2q", (0, 512), T.l2[:, 8:9], c_l)
-    fan_codes("v2q", "lwq", "win", wv, who=(2,))
-    fan_scales("v2q", "lwq", "win", ws, who=(2,))
-    wo = pick("lwq", 144, 192, "b2q", (0, 512), T.l2b[:, 0:3], c_l2)
-    c_ln3 = act(T.ln[:, 96:104], T.nbf[:, 8:16], F.Copy, c_nb, c_ln)
+    scores0(0, "zq", "b1q", wait=ZIN)
+    scores1(0, 192, "b1q", wait=ZIN)
+    for s in range(2):
+        for b in range(4):
+            if s == 0:
+                mm("mp", "pd%d" % b, r("epq", 128 * b, 128 * b + 128), r("zq", 0, 256), True, True, wait=ZIN)
+            if b < 2:
+                copy("dq", r("dq", 256 * b + 128 * s, 256 * b + 128 + 64 * s), unpacked(b, s), "sv")
+        if s == 0:
+            for k in range(6):
+                word(0, k)
+    lists(0, "psa", "psb")
+    numbers(0)
+    fill("nbz", r("nbf", 8, 16, p=(64, 128)), 0.0, "sv")
+    fill("wt", r("wt"), -1.0, "sv")
+    pick("va", r("vbq", 0, 128), r("p1q"), r("l1", 0, 8))
+    pick("vb", r("vbq", 128, 192), r("p1q"), r("l1", 8, 12))
+    send("v", "vbq", (0, 48, 144), "lvq", BACK, "vin")
+    for b in range(4):
+        rest(b, 0)
+    quant("raq", r("raq"), r("rt", 0, 512))
+    for b in range(4):
+        rest(b, 1)
+    scores0(1, "raq", "b2q")
+    quant("rcq", r("zq", 320, 448), r("rt", 512, 1024))
+    scores1(1, 320, "b2q")
+    for k in range(6):
+        word(1, k)
+    lists(1, "psb", "psc")
+    numbers(1)
+    fan("n", [r("nbf", 8 * (a // 2), 8 * (a // 2) + 8) for a in ALL], [r("ln", 32 * (2 - a), 32 * (2 - a) + 8) for a in ALL], "nin")
+    pick("wa", r("v2q", 0, 96), r("b2q"), r("l2", 0, 6))
+    pick("wb", r("v2q", 96, 160), r("b2q"), r("l2", 8, 12))
+    WIN = []
+    for k, who in enumerate(((0, 1), (2,))):
+        send("w", "v2q", (0, 48, 112), "lwq", BACK, "win%d" % k, who=who)
+        WIN.append(("win%d" % k, 2 * lands(who)))
 
-    vo = pick("lvq", 144, 192, "p1q", (0, 128), T.l1b[:, 0:3], c_lb)
-    c_q = quant(T.wq[:], T.wqs[:], T.wb[:], ("dw", 16))
-    ov, os_ = pick("o1q", 0, 192, "lvq", (0, 208), T.pl[:, 0:12], c_pl, ("vin", 2 * landing), vo[0], vo[1], ("dz", 64))
-    need("y", ov, os_)
-    dma("y", T.oc[:, 0:768], T.o1q[:].bitcast(dt.uint8), "st")
+    VIN = [("vin", 2 * landing)]
+    pick("vo", r("lvq", LAND + 144, LAND + 192), r("p1q"), r("l1", 6, 9))
+    quant("wq", r("wq"), r("wb"))
+    pick("o1", r("o1q"), r("lvq"), r("pl"), wait=VIN)
+    step("oc", "ys", lambda q: eng[q].dma_start(T.oc[:, 0:768], T.o1q[:].bitcast(dt.uint8)), [r("o1q")], [], sem="st")
     for k in range(4):
-        dma("y", T.osc[4 * k:4 * k + 4, 0:192], T.o1qs[32 * k:32 * k + 4, :], "st")
-    mm(T.psc[:, 0:192], "wq", 0, 128, "o1q", 0, 192, True, False, c_q, ov, os_, vc)
-    need("v", c_ln3, ("nin", landing))
-    c = done("v", V.transpose(T.tr[:], T.ln[:]))
-    c_t = []
-    for k, (a, q, i, n, o) in enumerate(((0, 1, 0, 32, 0), (0, 2, 0, 16, 32), (1, 1, 16, 16, 0), (1, 2, 0, 32, 16),
-                                         (2, 0, 0, 32, 0), (2, 1, 0, 16, 32), (3, 2, 16, 16, 0), (3, 3, 0, 32, 16))):
-        out, in_ = T.wt[0:32, 48 * a + o:48 * a + o + n], T.tr[32 * q:32 * q + 32, 32 * a + i:32 * a + i + n]
-        c_t.append(act(out, in_, F.Copy, c, c_wt) if k % 3 == 1 else copy(out, in_, c, c_wt))
-    ov, os_ = pick("o2q", 0, 192, "lwq", (0, 208), T.pl[:, 0:12], ("win", 2 * lands((0, 1), (2,))), wo[0], wo[1])
-    m = mm(T.psc[:, 0:192], "wq", 0, 128, "o2q", 0, 192, False, True, ov, os_)
-    need("y", ov)
-    dma("y", T.oc[:, 768:1536], T.o2q[:].bitcast(dt.uint8), "st")
-    need("s", os_)
+        dma("os", "ys", T.osc[4 * k:4 * k + 4, 0:192], r("o1qs", p=(32 * k, 32 * k + 4)), "st")
+    mm("my", "pd1", r("wq"), r("lvq", 128, 272), True, False, wait=VIN)
+    mm("my", "psd", r("wq"), r("lvq", 80, 208), True, False, wait=VIN)
+    fill("yz", r("yl", 0, LAND), 0.0)
+    pick("wo", r("lwq", LAND + 144, LAND + 192), r("b2q"), r("l2", 6, 9))
+    copy("ln", r("ln", 96, 104, p=(96, 128)), r("nbf", 0, 8, p=(96, 128)), "sv")
+    copy("ln", r("ln", 96, 104, p=(0, 32)), r("nbf", 8, 16, p=(0, 32)), "sv")
+    step("tr", "v", lambda q: V.transpose(T.tr[:], T.ln[:]), [r("ln")], [r("tr")], wait=[("nin", landing)])
+    for a, q, i, n, o in ((0, 0, 16, 16, 0), (0, 1, 0, 32, 16), (1, 1, 16, 16, 0), (1, 2, 0, 32, 16),
+                          (2, 0, 0, 32, 0), (2, 1, 0, 16, 32), (3, 3, 0, 32, 0), (3, 0, 0, 16, 32)):
+        o += LAND + 48 * a
+        copy("wc", r("wt", o, o + n, p=(0, 32)), r("tr", 32 * a + i, 32 * a + i + n, p=(32 * q, 32 * q + 32)))
+    copy("wno", r("wno"), by(r("wt"), r("pl")))
+    dma("wn", "ys", T.wn[:], r("wno", p=(0, 8)), "st")
+    pick("o2", r("o2q"), r("lwq"), r("pl"), wait=WIN)
+    mm("mz", "pd1", r("wq"), r("lwq", 128, 272), False, True, wait=WIN[:1])
+    copy("yl", r("yl", 128, 272), r("pd1", 0, 144))
+    mm("mz", "psd", r("wq"), r("lwq", 80, 208), False, True, wait=WIN)
+    copy("yl", r("yl", 80, 128), r("psd", 0, 48))
+    for c in (0, 6):
+        copy("ysb", r("ysb", 16 * c, 16 * c + 96), by(r("yl"), r("pl", c, c + 6)))
+    step("oc", "ys", lambda q: eng[q].dma_start(T.oc[:, 768:1536], T.o2q[:].bitcast(dt.uint8)), [r("o2q")], [], sem="st")
     for k in range(4):
-        dma("s", T.osc[4 * k:4 * k + 4, 192:384], T.o2qs[32 * k:32 * k + 4, :], "st")
-    need("v", *c_t)
-    c_n = done("v", V.tensor_copy(T.wno[:], T.wt[:, 0:208].indirect(T.pl[:, 0:12])))
-    c = copy(T.ysb[:], T.psc[:, 0:192], m)
-    need("y", c_n)
-    dma("y", T.wn[:], T.wno[0:8, :], "st")
-    need("y", c)
-    dma("y", T.y[:], T.ysb[:], "st")
+        dma("os", "sy", T.osc[4 * k:4 * k + 4, 192:384], r("o2qs", p=(32 * k, 32 * k + 4)), "st")
+    dma("y", "ys", T.y[:], r("ysb"), "st")
 
-    need("y", *[(qsem[q], cnt[q]) for q in cnt])
-    need("y", ("st", 16 * stores[0]))
-    need("g", ("left", left[0]))
+    for k, s in enumerate(steps):
+        s["dep"] = {}
+        for e in steps[:k]:
+            if e["name"] in s["wait"] or any(_meet(a, b) for a in s["r"] for b in e["w"]) or \
+                    s["qs"] + e["qs"] != "tt" and any(_meet(a, b) for a in s["w"] for b in e["r"] + e["w"]):
+                s["dep"][e["name"]] = 1
+            elif any(a[0] == b[0] and a[0] in BANKS for a in s["r"] + s["w"] for b in e["r"] + e["w"]):
+                s["dep"][e["name"]] = 0
+    return steps, left[0]
+
+
+def rank_program(g, core, T, topo):
+    if T.rank_of(core) is None:
+        return
+    steps, left = steps_of(g, core, T, topo)
+    S = T.sem
+    eng = {"v": g.vector, "s": g.scalar, "t": g.tensor, "g": g, "y": g.sync}
+    at = {s["name"]: s for s in steps}
+    order = {q: [n for n in ORDER[q].split() if n in at] for q in eng}
+    mark, cnt, queue = {}, {}, {}
+    for q in eng:
+        for n in order[q]:
+            sem = at[n]["sem"] or "q" + q
+            cnt[sem] = cnt.get(sem, 0) + (16 if at[n]["sem"] else 1)
+            mark[n], queue[n] = (sem, cnt[sem]), q
+    assert len(mark) == len(steps)
+    known, after, pos = {q: {} for q in eng}, {}, {q: 0 for q in eng}
+
+    def need(q, sem, val, brings):
+        if known[q].get(sem, 0) < val:
+            eng[q].wait_ge(S[sem], val)
+            known[q][sem] = val
+            for k, v in brings.items():
+                known[q][k] = max(known[q].get(k, 0), v)
+    while len(after) < len(steps):
+        before = len(after)
+        for q in eng:
+            while pos[q] < len(order[q]) and all(d in after for d in at[order[q][pos[q]]]["dep"]):
+                s = at[order[q][pos[q]]]
+                deps = [d for d, raw in s["dep"].items() if raw or queue[d] != q or at[d]["sem"]]
+                for d in sorted(deps, key=lambda d: -mark[d][1]):
+                    if at[d]["sem"] != "left":
+                        need(q, mark[d][0], cnt[mark[d][0]] if at[d]["sem"] else mark[d][1], after[d])
+                for w in s["wait"]:
+                    if isinstance(w, tuple):
+                        need(q, w[0], w[1], {})
+                ins = s["make"](q)
+                if s["sem"] != "left":
+                    ins.then_inc(S[mark[s["name"]][0]], 16 if s["sem"] else 1)
+                after[s["name"]] = dict(known[q])
+                pos[q] += 1
+        assert len(after) > before
+    for sem in cnt:
+        if sem != "left":
+            need("y", sem, cnt[sem], {})
+    need("g", "left", left, {})

from concourse.bass import DstId, RemoteDMATransfer
from concourse.mybir import dt, AluOpType, AxisListType, ActivationFunctionType

A = AluOpType
F = ActivationFunctionType
NR = 4
OT = 944
LOW = -1e29
RND = 1.5 * 2.0 ** 27
LAND = 80
OPT = {}
ORDER = {
    "v": "zz gi zo ui tk vl cxc on df cxd ti e0 cxa e4 hi tk2 xq hcol off rsl off1 ua ih ofo rma trq eq eq1 mk hot1 hot epq2 otq epq1 p1q "
         "epq3 rr b1q3 hc tk1 wl1 nl bb1 bb aa aa1 aa3 aa2 epq abq b1q2 wl2 b1q zl wl wl3 zsc ph1 zo1 ph bm22 zo2 pg1 wlq xpq zoc b1q1 "
         "zq pl rm rm2 rm3 rm1 b2q1 rm4 rm5 hixaq loxaq b2q2 xaq hixcq b2q loxcq b2q3 l1 xcq rg rg1 ra l11 ra1 rg2 raq rg3 ra2 ra3 vbc "
         "rcq rm8 rm9 rm6 rm7 vac rm10 rm11 hixaq1 nbz loxaq1 nb3 xaq1 hixcq1 nb5 loxcq1 wq xcq1 l2 voc wac l21 ln2 wbc tr wc9 wc6 wc5 "
         "wc3 wc4 wc8 woc o1c o2c yl1 ysb1",
    "s": "co cxb trb epb wlb nf bm13 bm12 bm1 db1 db3 db zss pg bm11 zos bm21 db2 sg sg2 sg3 sg1 sg5 sg4 dq dq2 dq1 gs gs1 dq3 nb1 gs2 "
         "gs3 nb2 vas vbs vos nb sg8 sg9 sg6 sg7 sg10 sg11 nb4 o1s was ln1 wos wbs wc2 wc7 os wno yl o2s ysb os7 os4",
    "t": "mc mc1 mu mt mb2 mb1 mb3 ml mb mxpq mxpq1 ma ma2 ma1 mh mh1 mp3 mp2 mp mp1 mxaq mxaq1 mxcq mxcq1 ma5 ma3 ma4 mh2 mh3 mxaq2 "
         "mxaq3 mxcq2 mxcq3 my mz my1 mz1",
    "g": "pi im iba rst cel t1 ibb tri eye ofs m16 ln zc zs bm2 bm23 rz wt yz vs vc n wc ws wc1 ws1",
    "y": "x b1 b2 dz3 dz dz2 dz1 ofa w wn oc os1 os2 os3 oc1 os5 os6 y",
}


def _sb(n, d):
    return ("sbuf", [128, n], d)


SCRATCH = {}
for _n, _w in (("xq", 236), ("wq", 128), ("b1q", 512), ("b2q", 512), ("trq", 128), ("wlq", 128), ("epq", 512), ("p1q", 128),
               ("otq", 128), ("abq", 140), ("xaq", 136), ("xcq", 132), ("xpq", 140), ("zsq", 144), ("zq", 448), ("vbq", 192),
               ("lvq", 272), ("v2q", 160), ("lwq", 272), ("raq", 128), ("o1q", 192), ("o2q", 192)):
    SCRATCH[_n] = _sb(_w, "float8_e4m3fn_x4")
    SCRATCH[_n + "s"] = _sb(_w, "uint8")
for _n, _w in (("cx", 1024), ("wb", 512), ("pp", 640), ("pq", 512), ("bm1", 2048), ("bm2", 2048), ("trb", 512), ("wlb", 512),
               ("epb", 516), ("ab", 656), ("rt", 1024), ("zz", 536), ("on1", 128), ("m16", 12),
               ("t1", 128), ("im", 128), ("ih", 128), ("jk1", 768), ("jk2", 768), ("nbf", 16), ("ln", 128), ("tr", 128)):
    SCRATCH[_n] = _sb(_w, "bfloat16")
for _n, _w in (("rst", 10), ("rma", 10), ("ua", 11), ("rr", 10), ("hc", 2), ("tk", 3), ("ib", 24),
               ("vl", 1), ("mk", 4), ("hcol", 1), ("df", 1), ("e0", 1), ("e4", 1), ("off", 2), ("rm1", 768), ("rm2", 768), ("nf", 128),
               ("wt", 272), ("wno", 192), ("ysb", 192), ("yl", 272), ("db", 512), ("dq", 512), ("gs", 1024)):
    SCRATCH[_n] = _sb(_w, "float32")
for _n, _w in (("pi", 1), ("gi", 1), ("ui", 1), ("ti", 1), ("hi", 1), ("t2", 1)):
    SCRATCH[_n] = _sb(_w, "int32")
for _n, _w in (("zl", 12), ("zl2", 8), ("pl", 12), ("l1", 12), ("l2", 12), ("ofo", 2), ("ofa", 8)):
    SCRATCH[_n] = _sb(_w, "uint16")
BANKS = ("psa", "psb", "psc", "psd", "pd0", "pd1", "pd2", "pd3")
for _n in BANKS:
    SCRATCH[_n] = ("psum", [128, 512], "float32")
SEMAPHORES = ["qv", "qs", "qt", "qg", "dx", "dco", "dp1", "db2", "dw", "do", "dz", "st", "zin", "vin", "win0", "win1", "nin", "oin", "left"]


def _mask(topo, src, peers, kind, who):
    out, far = {}, 0
    for k, a in enumerate(who):
        c = peers[a]
        e = topo.engines(src, c)
        if len(who) < 3:
            out[c] = e[k::len(who)]
        elif topo.die(src) != topo.die(c):
            out[c] = e[far * 8 + kind:far * 8 + 8:2]
            far += 1
        else:
            out[c] = e[1 - kind::2]
    return out


def r(name, c0=0, c1=None, step=1, p=(0, 128)):
    return (name, c0, SCRATCH[name][1][1] if c1 is None else c1, step, p, None)


def by(win, off):
    return win[:5] + (off,)


def _meet(a, b):
    return a[0] == b[0] and a[4][0] < b[4][1] and b[4][0] < a[4][1] and not set(range(*a[1:4])).isdisjoint(range(*b[1:4]))


def steps_of(g, core, T, topo):
    rank = T.rank_of(core)
    S = T.sem
    V, SC, TE = g.vector, g.scalar, g.tensor
    eng = {"v": V, "s": SC, "t": TE, "g": g, "y": g.sync}
    steps, names = [], {}

    def ap(x, cast=None):
        if not isinstance(x, tuple):
            return x
        v = T[x[0]][x[4][0]:x[4][1], x[1]:x[2]:x[3]] if x[3] > 1 else T[x[0]][x[4][0]:x[4][1], x[1]:x[2]]
        if cast is not None:
            v = v.bitcast(cast)
        return v if x[5] is None else v.indirect(ap(x[5]))

    def step(name, qs, make, reads, writes, wait=(), sem=None):
        names[name] = names.get(name, -1) + 1
        reads = [x for x in reads if isinstance(x, tuple)]
        reads += [x[5] for x in reads if x[5] is not None]
        steps.append({"name": name + (str(names[name]) if names[name] else ""), "qs": qs, "make": make, "r": reads,
                      "w": [x for x in writes if isinstance(x, tuple)], "wait": list(wait), "sem": sem})
        return steps[-1]["name"]

    def dma(name, qs, out, in_, sem, cast=None, **k):
        return step(name, qs, lambda q: eng[q].dma_start(ap(out, cast), ap(in_, cast)), [in_], [out], sem=sem, **k)

    def ts(name, out, in0, s1, s2, op0, op1=None, **k):
        ops = (op0,) if op1 is None else (op0, op1)
        return step(name, "v", lambda q: V.tensor_scalar(ap(out), ap(in0), ap(s1), ap(s2), *ops), [in0, s1, s2], [out], **k)

    def tt(name, out, a, b, op, **k):
        return step(name, "v", lambda q: V.tensor_tensor(ap(out), ap(a), ap(b), op), [a, b], [out], **k)

    def times(name, out, in_, c, edge=None):
        def make(q):
            if q == "g":
                return g.affine_select(ap(out), ap(in_), [[0, 512]], A.is_ge, 0.0, *edge)
            if q == "s":
                return SC.activation(ap(out), ap(in_), F.Copy, scale=ap(c))
            return V.tensor_scalar(ap(out), ap(in_), ap(c), None, A.mult)
        return step(name, "svg" if edge else "sv", make, [in_, c], [out])

    def fill(name, out, c, qs="vs"):
        z = r("zz", 0, len(range(*out[1:4])), p=out[4])

        def make(q):
            if q == "g":
                return g.iota(ap(out), [[0, z[2]]], int(c), 0, allow_small_or_imprecise_dtypes=True)
            return V.memset(ap(out), c) if q == "v" else SC.activation(ap(out), ap(z), F.Identity, bias=c)
        return step(name, qs + "g" if len(qs) > 1 and c == int(c) and out[4] == (0, 128) else qs, make, [z] if "s" in qs else [], [out])

    def copy(name, out, in_, qs="vs", **k):
        return step(name, qs, lambda q: V.tensor_copy(ap(out), ap(in_)) if q == "v" else SC.activation(ap(out), ap(in_), F.Copy),
                    [in_], [out], **k)

    def sc(x):
        return (x[0] + "s",) + x[1:]

    def quant(name, out, in_, **k):
        return step(name, "v", lambda q: V.quantize_mx(ap(out), ap(sc(out)), ap(in_)), [in_], [out, sc(out)], **k)

    def iota(name, out, pattern, base):
        return step(name, "g", lambda q: g.iota(ap(out), pattern, base, 0, allow_small_or_imprecise_dtypes=True), [], [out])

    def select(name, out, in_, pattern, op, c):
        return step(name, "g", lambda q: g.affine_select(ap(out), ap(in_), pattern, op, c, 0, -1), [in_], [out])

    def scan(name, out, d0, d1, first=LOW):
        return step(name, "v", lambda q: V.tensor_tensor_scan(ap(out), ap(d0), ap(d1), first, A.add, A.max), [d0, d1], [out])

    def mm(name, bank, a, b, start, stop, **k):
        out = r(bank, 0, b[2] - b[1])
        return step(name, "t", lambda q: TE.matmul_mx(ap(out), ap(a), ap(sc(a)), ap(b), ap(sc(b)), start, stop),
                    [a, sc(a), b, sc(b)], [out], **k)

    def pick(name, out, win, lst, **k):
        step(name + "c", "v", lambda q: V.tensor_copy(ap(out, dt.uint32), ap(by(win, lst), dt.uint32)), [by(win, lst)], [out], **k)
        copy(name + "s", sc(out), by(sc(win), lst), qs="sv", **k)

    ALL = (0, 1, 2)
    peers = [T.cores[(rank + 1 + a) % NR] for a in ALL]

    def lands(who):
        return sum(len(_mask(topo, c, [T.cores[(T.rank_of(c) + 1 + a) % NR] for a in ALL], 0, who).get(core, ())) for c in peers)
    landing = lands(ALL)
    left = [0]

    def fan(name, srcs, dsts, sem, cast=None, kind=0, who=ALL, **k):
        emask = _mask(topo, core, peers, kind, who)
        tr = []
        for a in who:
            c = peers[a]
            rid, pid, _ = topo.addr(c)
            tr.append(RemoteDMATransfer(dst_ids=[DstId(rid=rid, pnc=pid)], dma_engine_mask=sum(1 << e for e in emask[c]),
                                        remote_sem=S[sem], srcs=[ap(srcs[a], cast)], dsts=[ap(dsts[a], cast)]))
            left[0] += len(emask[c])
        return step(name, "g", lambda q: g.remote_dma_fused(tr, local_sem=S["left"]), [srcs[a] for a in who], [], sem="left", **k)

    def send(name, src, at, dst, to, sem, who=ALL, **k):
        s, d = [r(src, at[a], at[a] + 48) for a in ALL], [r(dst, to[2 - a], to[2 - a] + 48) for a in ALL]
        fan(name + "c", s, d, sem, cast=dt.uint8, who=who, **k)
        fan(name + "s", [sc(x) for x in s], [sc(x) for x in d], sem, kind=1, who=who, **k)
    BACK = (LAND, LAND + 48, LAND + 96)

    dma("x", "y", r("cx", 128, 896), T.x[:], "dx")
    dma("co", "s", r("cx", 24, 40), T.co[:, 0:4 * NR], "dco")
    dma("b1", "y", r("pp", 96, 608), T.b1[:], "dp1")
    dma("b2", "y", r("pq"), T.b2[:], "db2")

    step("pi", "g", lambda q: g.iota(T.pi[:], [[0, 1]], 0, 1), [], [r("pi")])
    fill("zz", r("zz"), 0.0, "v")
    fill("on", r("on1"), 1.0)
    fill("trb", r("trb"), 1.0, "sv")
    fill("ua", r("ua"), 0.0, "sv")
    fill("nf", r("nf"), 0.0, "sv")
    fill("epb", r("epb"), 0.0, "sv")
    select("t1", r("t1"), r("on1"), [[1, 128]], A.is_gt, 0.0)
    iota("im", r("im"), [[0, 8], [1, 16]], 0)
    step("ih", "sv", lambda q: SC.activation(T.ih[:], T.im[:], F.Identity, bias=-7.5) if q == "s" else
         V.tensor_scalar(T.ih[:], T.im[:], -7.5, None, A.add), [r("im")], [r("ih")])
    fill("wlb", r("wlb"), 0.0, "sv")
    c_ln = fill("ln", r("ln"), 0.0, "sv")
    if rank < NR - 1:
        iota("iba", r("ib", 0, 18 - 6 * rank), [[256, 3 - rank], [16, 3], [0, 2]], 1280 + 256 * rank)
    iota("ibb", r("ib", 18 - 6 * rank, 24), [[256, rank + 1], [16, 3], [0, 2]], 1024)
    ts("gi", r("gi"), r("pi"), 4, None, A.arith_shift_right)
    ts("ui", r("ui"), r("pi"), 2, 3, A.arith_shift_right, A.bitwise_and)
    ts("ti", r("ti"), r("pi"), (3, 1, 0, 0)[rank], None, A.bitwise_and)
    ts("hi", r("hi"), r("pi"), 5, None, A.arith_shift_right)
    tt("df", r("df"), r("gi"), r("ui"), A.subtract)
    fill("cxa", r("cx", 0, 24), 0.0)
    ts("hcol", r("hcol"), r("hi"), 128.0, None, A.mult)
    if rank == 1:
        ts("e0", r("t2"), r("pi"), 1, 1, A.arith_shift_right, A.bitwise_and)
        ts("e4", r("e4"), r("t2"), 4.0, r("df"), A.mult, A.is_equal)
    else:
        if rank < 3:
            ts("e0", r("e0"), r("df"), 0.0, None, A.is_equal)
        ts("e4", r("e4"), r("df"), 4.0, None, A.is_equal)
    fill("cxb", r("cx", 40, 128), 0.0)
    fill("cxc", r("cx", 896, OT + 80), 0.0)
    none = (8.0, 8.0, 24.0, 24.0)[rank]
    for k, e in enumerate((("e0", "e4"), ("e4",))[rank % 2]):
        ts("off", r("off", k, k + 1), r("ti"), (0.0, 4.0, 11.0, 23.0)[rank] - none, r(e), A.add, A.mult)
    wide = 2 - rank % 2
    fill("rst", r("rst"), 0.0)
    ts("ofo", r("ofo", 0, wide), r("off", 0, wide), none, None, A.add)
    fill("rsl", r("rst", 4, 7), LOW, "v")
    ts("mk", r("mk"), r("im", 0, 4), 128.0, r("hcol"), A.mult, A.is_equal)
    ts("vl", r("vl"), r("pi"), 64.0, None, A.is_ge)
    fill("cxd", r("cx", 898, OT, 4), -7.5 / 128)
    quant("zq", r("zq", 256, 384), r("zz", 0, 512))
    select("tri", r("trb", 0, 512, 4), r("t1"), [[1, 128]], A.not_equal, 1024.0)
    iota("cel", r("cx", 899, OT, 4), [[0, 2], [2, 6]], 0)
    fan("ofs", [r("ofo", 0, wide)] * 3, [r("ofa", 2 * rank, 2 * rank + wide)] * 3, "oin")
    OIN = [("oin", landing), dma("ofa", "y", r("ofa", 2 * rank, 2 * rank + wide), r("ofo", 0, wide), "do")]
    select("eye", r("epb", 4, 516, 4), r("on1"), [[1, 128]], A.is_equal, 0.0)
    EDGE = {0: (31, -1), 3: (-96, 1)}
    for h in range(4):
        times("bm1", r("bm1", 512 * h, 512 * h + 512), r("pp", 96, 608), r("mk", h, h + 1), EDGE.get(h))
    for h in range(4):
        times("bm2", r("bm2", 512 * h, 512 * h + 512), r("pq"), r("mk", h, h + 1), EDGE.get(h))

    quant("xq", r("xq"), r("cx", 0, OT))
    for b in ("lvq", "lwq"):
        dma("dz", "y", r(b, 0, 16), r("xq", 16, 32), "dz", cast=dt.uint8)
        dma("dz", "y", r(b + "s", 0, 16), r("xqs", 16, 32), "dz")
    mm("mc", "psa", r("xq", 32, 160), r("xq", 6, 134), True, False)
    mm("mc", "psa", r("xq", 96, 224), r("xq", 0, 128), False, True)
    quant("trq", r("trq"), r("trb"))
    scan("rma", r("rma"), r("rst"), r("psa", 0, 10))
    ts("eq", r("ua", 1, 5), r("rma", 0, 4), r("rma", 3, 4), None, A.is_equal)
    ts("eq", r("ua", 7, 11), r("rma", 6, 10), r("rma", 9, 10), r("vl"), A.is_equal, A.mult)
    tt("hot", r("cx", OT + 24, OT + 64, 4), r("ua", 1, 11), r("ua", 0, 10), A.subtract)
    tt("hot", r("cx", OT + 49, OT + 64, 4), r("ua", 1, 5), r("ua", 0, 4), A.subtract)
    quant("otq", r("otq"), r("cx", OT + 64 - 512, OT + 64))
    mm("mu", "psc", r("trq"), r("xq", 106, 234), True, False)
    mm("mt", "psc", r("trq"), r("otq"), False, True)
    ts("tk", r("tk", 0, 1), r("gi"), 16.0, None, A.mult)
    ts("tk", r("tk", 1, 2), r("gi"), 16.0, 64.0, A.mult, A.add)
    tt("tk", r("tk", 2, 3), r("pi"), r("tk", 0, 1), A.subtract)
    fill("m16", r("m16"), -16.0)
    scan("rr", r("rr"), r("rst"), r("psc", 118, 128))
    ts("hc", r("hc"), r("rr", 3, 10, 6), RND, RND, A.add, A.subtract)
    tt("nl", r("nf", 107, 120, 12), r("rr", 3, 10, 6), r("hc"), A.subtract)
    for s in range(2):
        ts("bb", r("ab", 512 + s, 560, 2), r("ib"), r("hc", s, s + 1), 256.0, A.is_equal, A.mult)
    for t in range(4):
        k = 107 + 12 * (t % 2)
        ts("aa", r("ab", t, 512, 4), r("ih"), r("nf", k, k + 1), r("tk", min(t, 2), min(t, 2) + 1), A.is_equal, A.mult)
    quant("abq", r("abq"), r("ab", 0, 560))
    mm("ml", "psa", r("abq", 0, 128), r("abq", 12, 140), True, True)
    ts("zl", r("zl", 0, 9), r("psa", 116, 125), 1.0 / 256, None, A.mult)
    pick("zs", r("zsq"), r("xq", 32, 224), r("zl", 0, 9))
    send("z", "zsq", (0, 48, 96), "zq", (0, 48, 208), "zin", wait=[c_ln])
    ZIN = [("zin", 2 * landing)]
    fill("rz", r("rt", 768, 1024), 0.0)
    fill("zo", r("zl2", 2, 6), 16, "v")
    ts("zo", r("zl2", 0, 2), r("psa", 125, 127), 1.0 / 256, 32.0, A.mult, A.add)
    ts("zo", r("zl2", 6, 7), r("psa", 127, 128), 1.0 / 256, 32.0, A.mult, A.add)
    pick("zo", r("zq", 96, 208), r("xq", 0, 224), r("zl2", 0, 7))
    for h in range(4):
        quant("b1q", r("b1q", 128 * h, 128 * h + 128), r("bm1", 512 * h, 512 * h + 512))
    dma("w", "y", r("wb"), T.w[:], "dw", wait=ZIN)
    for t in range(4):
        ts("wl", r("wlb", 129 * t, 128 * t + 128, 4), r("im", 0, 32), r("tk", 2, 3), None, A.is_equal)
    quant("wlq", r("wlq"), r("wlb"))
    for b in range(4):
        quant("epq", r("epq", 128 * b, 128 * b + 128), r("epb", 4 - b, 516 - b))
    quant("p1q", r("p1q"), r("pp", 96, 608))
    for b in range(4):
        mm("mb", "pd%d" % b, r("epq", 128 * b, 128 * b + 128), r("p1q"), True, True)
        times("db", r("db", 128 * b, 128 * b + 128), r("pd%d" % b, 0, 128), -1.0)
    for h in range(4):
        quant("b2q", r("b2q", 128 * h, 128 * h + 128), r("bm2", 512 * h, 512 * h + 512))

    banks = (("psa", "psb", "psc", "psd"), ("pd2", "pd3", "psa", "pd0"))
    NH, NL = 64, 96
    O0, O1, OP = r("ofa", 0, 2), r("ofa", 2, 3), r("ofa", 4, 7)

    def scores0(lv, tok, bk, **k):
        for h in range(3):
            mm("ma", banks[lv][h], r(tok, 0, 128), r(bk, 128 * h, 128 * h + 128 + 128 * (h // 2)), True, True, **k)

    def scores1(lv, c0, bk, **k):
        mm("mh", banks[lv][3], r("zq", c0, c0 + 128), r(bk, 0, 256), True, False, **k)
        mm("mh", banks[lv][3], r("zq", c0 - 64, c0 + 64), r(bk, 256, 512), False, True, **k)

    def word(lv, k):
        e, rm, jk = 128 * k, "rm%d" % (lv + 1), "jk%d" % (lv + 1)
        b, o = banks[lv][(0, 1, 2, 2, 3, 3)[k]], (0, 0, 0, 128, 0, 128)[k]
        at = 32 * lv + 16 * (k // 4) + k
        run, top, fl, n = r(rm, e, e + 128), r(rm, e + 127, e + 128), r(jk, e, e + 128), r("nf", at, at + 1)
        scan("rm", run, r("zz", 0, 128), r(b, o, o + 128))
        step("sg", "s", lambda q: SC.activation(ap(fl), ap(run), F.Sign, bias=ap(top), scale=-1.0, accum_out=ap(n)), [run], [fl, n])

    def tolist(at, off, buf, o, w0, xt, bank):
        n = 16 * (off[2] - off[1])
        win = by(r("nf", at, at + 16), off)
        ts("hi" + xt, r(buf, o, o + n), win, RND, RND, A.add, A.subtract, wait=OIN)
        tt("lo" + xt, r(buf, o + n, o + 2 * n), win, r(buf, o, o + n), A.subtract, wait=OIN)
        added(buf, w0, xt, n // 4, bank)

    def added(buf, w0, xt, w, bank):
        quant(xt, r(xt, 0, 128 + w), r(buf, w0, w0 + 512 + 4 * w))
        mm("m" + xt, bank, r("wlq"), r(xt, 0, 128), True, False)
        mm("m" + xt, bank, r("wlq"), r(xt, w, 128 + w), False, True)

    def listed(lv, dst, src):
        if lv == 0:
            copy("l1", dst, src, "v")
        else:
            ts("l2", dst, src, r("hcol"), None, A.add)

    def lists(lv, ba, bc):
        l = "l%d" % (lv + 1)
        tolist(32 * lv, O0, "pp", 32, 32, "xaq", ba)
        listed(lv, r(l, 0, 8), r(ba, 0, 8))
        tolist(32 * lv + 16, O1, "pp", 608, 112, "xcq", bc)
        listed(lv, r(l, 8, 12), r(bc, 124, 128))

    def unpacked(b, s):
        return r("pd%d" % b, 192 * s, 128 + 128 * s)

    def rest(b, s):
        out, lst = r("rt", 512 * s + b, 512 + 256 * s, 4), r("l1", 8 * s, 8 + 4 * s)
        tab, o = by(r("db", 128 * b, 128 * b + 128), lst), 256 * b + 128 * s
        if b < 2:
            tt("rg", out, tab, r("dq", o, o + 128 - 64 * s), A.add)
        else:
            copy("gs", r("gs", o, o + 128 - 64 * s), tab, "sv")
            tt("ra", out, r("gs", o, o + 128 - 64 * s), unpacked(b, s), A.add)

    def numbers(lv):
        c = 32 * lv + 20
        copy("nb", r("nbf", 4 * lv, 4 * lv + 4), r("nf", 32 * lv, 32 * lv + 4), "sv")
        copy("nb", r("nbf", 8 + 4 * lv, 10 + 4 * lv, p=(0, 64)), r("nf", c, c + 2, p=(0, 64)), "sv")
        copy("nb", r("nbf", 10 + 4 * lv, 12 + 4 * lv, p=(0, 64)), r("nf", c, c + 2, p=(64, 128)), "sv")

    for s in range(2):
        scan("ph", r("nf", NH + 12 * s, NH + 12 * s + 12), r("m16"), r("ab", 512 + s, 560, 4), first=0.0)
    copy("pg", r("ab", 608, 656), by(r("nf", NL, NL + 32), OP), wait=OIN)
    copy("pg", r("ab", 560, 608), by(r("nf", NH, NH + 32), OP), wait=OIN)
    added("ab", 96, "xpq", 12, "psd")
    ts("pl", r("pl"), r("psd", 116, 128), 7.5, None, A.add)

    scores0(0, "zq", "b1q", wait=ZIN)
    scores1(0, 192, "b1q", wait=ZIN)
    for s in range(2):
        for b in range(4):
            if s == 0:
                mm("mp", "pd%d" % b, r("epq", 128 * b, 128 * b + 128), r("zq", 0, 256), True, True, wait=ZIN)
            if b < 2:
                copy("dq", r("dq", 256 * b + 128 * s, 256 * b + 128 + 64 * s), unpacked(b, s), "sv")
        if s == 0:
            for k in range(6):
                word(0, k)
    lists(0, "psa", "psb")
    numbers(0)
    fill("nbz", r("nbf", 8, 16, p=(64, 128)), 0.0, "sv")
    fill("wt", r("wt"), -1.0, "sv")
    pick("va", r("vbq", 0, 128), r("p1q"), r("l1", 0, 8))
    pick("vb", r("vbq", 128, 192), r("p1q"), r("l1", 8, 12))
    send("v", "vbq", (0, 48, 144), "lvq", BACK, "vin")
    for b in range(4):
        rest(b, 0)
    quant("raq", r("raq"), r("rt", 0, 512))
    for b in range(4):
        rest(b, 1)
    scores0(1, "raq", "b2q")
    quant("rcq", r("zq", 320, 448), r("rt", 512, 1024))
    scores1(1, 320, "b2q")
    for k in range(6):
        word(1, k)
    lists(1, "psb", "psc")
    numbers(1)
    fan("n", [r("nbf", 8 * (a // 2), 8 * (a // 2) + 8) for a in ALL], [r("ln", 32 * (2 - a), 32 * (2 - a) + 8) for a in ALL], "nin")
    pick("wa", r("v2q", 0, 96), r("b2q"), r("l2", 0, 6))
    pick("wb", r("v2q", 96, 160), r("b2q"), r("l2", 8, 12))
    WIN = []
    for k, who in enumerate(((0, 1), (2,))):
        send("w", "v2q", (0, 48, 112), "lwq", BACK, "win%d" % k, who=who)
        WIN.append(("win%d" % k, 2 * lands(who)))

    VIN = [("vin", 2 * landing)]
    pick("vo", r("lvq", LAND + 144, LAND + 192), r("p1q"), r("l1", 6, 9))
    quant("wq", r("wq"), r("wb"))
    pick("o1", r("o1q"), r("lvq"), r("pl"), wait=VIN)
    step("oc", "ys", lambda q: eng[q].dma_start(T.oc[:, 0:768], T.o1q[:].bitcast(dt.uint8)), [r("o1q")], [], sem="st")
    for k in range(4):
        dma("os", "ys", T.osc[4 * k:4 * k + 4, 0:192], r("o1qs", p=(32 * k, 32 * k + 4)), "st")
    mm("my", "pd1", r("wq"), r("lvq", 128, 272), True, False, wait=VIN)
    mm("my", "psd", r("wq"), r("lvq", 80, 208), True, False, wait=VIN)
    fill("yz", r("yl", 0, LAND), 0.0)
    pick("wo", r("lwq", LAND + 144, LAND + 192), r("b2q"), r("l2", 6, 9))
    copy("ln", r("ln", 96, 104, p=(96, 128)), r("nbf", 0, 8, p=(96, 128)), "sv")
    copy("ln", r("ln", 96, 104, p=(0, 32)), r("nbf", 8, 16, p=(0, 32)), "sv")
    step("tr", "v", lambda q: V.transpose(T.tr[:], T.ln[:]), [r("ln")], [r("tr")], wait=[("nin", landing)])
    for a, q, i, n, o in ((0, 0, 16, 16, 0), (0, 1, 0, 32, 16), (1, 1, 16, 16, 0), (1, 2, 0, 32, 16),
                          (2, 0, 0, 32, 0), (2, 1, 0, 16, 32), (3, 3, 0, 32, 0), (3, 0, 0, 16, 32)):
        o += LAND + 48 * a
        copy("wc", r("wt", o, o + n, p=(0, 32)), r("tr", 32 * a + i, 32 * a + i + n, p=(32 * q, 32 * q + 32)))
    copy("wno", r("wno"), by(r("wt"), r("pl")))
    dma("wn", "ys", T.wn[:], r("wno", p=(0, 8)), "st")
    pick("o2", r("o2q"), r("lwq"), r("pl"), wait=WIN)
    mm("mz", "pd1", r("wq"), r("lwq", 128, 272), False, True, wait=WIN[:1])
    copy("yl", r("yl", 128, 272), r("pd1", 0, 144))
    mm("mz", "psd", r("wq"), r("lwq", 80, 208), False, True, wait=WIN)
    copy("yl", r("yl", 80, 128), r("psd", 0, 48))
    for c in (0, 6):
        copy("ysb", r("ysb", 16 * c, 16 * c + 96), by(r("yl"), r("pl", c, c + 6)))
    step("oc", "ys", lambda q: eng[q].dma_start(T.oc[:, 768:1536], T.o2q[:].bitcast(dt.uint8)), [r("o2q")], [], sem="st")
    for k in range(4):
        dma("os", "sy", T.osc[4 * k:4 * k + 4, 192:384], r("o2qs", p=(32 * k, 32 * k + 4)), "st")
    dma("y", "ys", T.y[:], r("ysb"), "st")

    for k, s in enumerate(steps):
        s["dep"] = {}
        for e in steps[:k]:
            if e["name"] in s["wait"] or any(_meet(a, b) for a in s["r"] for b in e["w"]) or \
                    s["qs"] + e["qs"] != "tt" and any(_meet(a, b) for a in s["w"] for b in e["r"] + e["w"]):
                s["dep"][e["name"]] = 1
            elif any(a[0] == b[0] and a[0] in BANKS for a in s["r"] + s["w"] for b in e["r"] + e["w"]):
                s["dep"][e["name"]] = 0
    return steps, left[0]


def rank_program(g, core, T, topo):
    if T.rank_of(core) is None:
        return
    steps, left = steps_of(g, core, T, topo)
    S = T.sem
    eng = {"v": g.vector, "s": g.scalar, "t": g.tensor, "g": g, "y": g.sync}
    at = {s["name"]: s for s in steps}
    order = {q: [n for n in ORDER[q].split() if n in at] for q in eng}
    mark, cnt, queue = {}, {}, {}
    for q in eng:
        for n in order[q]:
            sem = at[n]["sem"] or "q" + q
            cnt[sem] = cnt.get(sem, 0) + (16 if at[n]["sem"] else 1)
            mark[n], queue[n] = (sem, cnt[sem]), q
    assert len(mark) == len(steps)
    known, after, pos = {q: {} for q in eng}, {}, {q: 0 for q in eng}

    def need(q, sem, val, brings):
        if known[q].get(sem, 0) < val:
            eng[q].wait_ge(S[sem], val)
            known[q][sem] = val
            for k, v in brings.items():
                known[q][k] = max(known[q].get(k, 0), v)
    while len(after) < len(steps):
        before = len(after)
        for q in eng:
            while pos[q] < len(order[q]) and all(d in after for d in at[order[q][pos[q]]]["dep"]):
                s = at[order[q][pos[q]]]
                deps = [d for d, raw in s["dep"].items() if raw or queue[d] != q or at[d]["sem"]]
                for d in sorted(deps, key=lambda d: -mark[d][1]):
                    if at[d]["sem"] != "left":
                        need(q, mark[d][0], cnt[mark[d][0]] if at[d]["sem"] else mark[d][1], after[d])
                for w in s["wait"]:
                    if isinstance(w, tuple):
                        need(q, w[0], w[1], {})
                ins = s["make"](q)
                if s["sem"] != "left":
                    ins.then_inc(S[mark[s["name"]][0]], 16 if s["sem"] else 1)
                after[s["name"]] = dict(known[q])
                pos[q] += 1
        assert len(after) > before
    for sem in cnt:
        if sem != "left":
            need("y", sem, cnt[sem], {})
    need("g", "left", left, {})
